import numpy as np
import ml_dtypes


def mxq(x, axis, fmt="e4m3"):
    dtype, down = {"e4m3": (ml_dtypes.float8_e4m3fn, 7), "e5m2": (ml_dtypes.float8_e5m2, 14)}[fmt]
    v = np.moveaxis(np.asarray(x, np.float32).astype(ml_dtypes.bfloat16).astype(np.float64), axis, -1)
    blocks = v.reshape(v.shape[:-1] + (-1, 32))
    amax = np.abs(blocks).max(-1, keepdims=True)
    byte = np.maximum(np.where(amax > 0, np.frexp(amax)[1] - 1 + 127, 0) - down, 1)
    scale = np.exp2(byte - 127.0)
    codes = (blocks / scale).astype(np.float32).astype(dtype).astype(np.float64)
    return np.moveaxis((codes * scale).reshape(v.shape), -1, axis)


WIDE = False


def mx_kscale(k):
    if not WIDE:
        return np.ones(k)
    levels = np.array([10, -10, 5, -5, 0])
    if k % 512:
        return np.exp2(np.random.permutation(np.resize(levels, k // 32))).repeat(32)
    a = np.empty((k // 512, 16))
    for p in range(k // 512):
        a[p, :8] = np.random.permutation(np.resize(levels, 8))
        for g in range(8):
            far = levels[np.abs(levels - a[p, g]) >= 10]
            a[p, g + 8] = far[np.random.randint(len(far))]
    return np.exp2(a.ravel()).repeat(32)


def f64(x):
    return np.asarray(x).astype(np.float64)


def striped(idx):
    return np.tile(np.asarray(idx).reshape(-1, 16).T, (8, 1)).astype(np.uint16)


def unstriped(offs):
    return offs[:16].T.reshape(-1).astype(np.int64)


E2M1 = np.array([0.0, 0.5, 1.0, 1.5, 2.0, 3.0, 4.0, 6.0, -0.0, -0.5, -1.0, -1.5, -2.0, -3.0, -4.0, -6.0])


def pack_weight(w, fmt):
    k, n = w.shape
    w = f64(np.asarray(w, np.float32).astype(ml_dtypes.bfloat16)).reshape(k // 32, 32, n)
    amax = np.abs(w).max(1)
    if fmt == "e4m3":
        byte = np.frexp(amax)[1] - 1 + 127 - 7
    else:
        mant, ex = np.frexp(amax / 6.0)
        byte = np.where(mant > 0.5, ex, ex - 1) + 127
    byte = np.clip(np.where(amax > 0, byte, 1), 1, 254)
    scaled = (w * np.exp2(127.0 - byte)[:, None, :]).reshape(k, n).astype(np.float32)
    by_word = np.ascontiguousarray(scaled.reshape(k // 512, 128, 4, n).transpose(0, 1, 3, 2))
    if fmt == "e4m3":
        words = by_word.astype(ml_dtypes.float8_e4m3fn).view(np.uint8)
    else:
        c = by_word.astype(ml_dtypes.float4_e2m1fn).view(np.uint8) & 0xF
        words = (c[..., 0::2] | (c[..., 1::2] << 4)).reshape(k // 512, 128, 2 * n)
    return np.ascontiguousarray(words), np.ascontiguousarray(byte.astype(np.uint8).reshape(k // 512, 16, n))


def unpack_weight(words, scales, fmt):
    g, _, n = scales.shape
    words = np.ascontiguousarray(words).reshape(g, 128, n, -1)
    if fmt == "e4m3":
        vals = words.view(ml_dtypes.float8_e4m3fn).astype(np.float64)
    else:
        nib = np.empty((g, 128, n, 4), np.uint8)
        nib[..., 0::2] = words & 0xF
        nib[..., 1::2] = words >> 4
        vals = E2M1[nib]
    vals = vals * np.repeat(np.exp2(scales.astype(np.float64) - 127.0), 8, axis=1)[..., None]
    return vals.transpose(0, 1, 3, 2).reshape(g * 512, n)


def bf(x):
    return np.asarray(x, np.float32).astype(ml_dtypes.bfloat16)


def planes(Y):
    r, m = Y.shape
    b = f64(bf(Y)).reshape(r // 32, 32, m)
    amax = np.abs(b).max(1)
    byte = np.clip(np.where(amax > 0, np.frexp(amax)[1] - 1 + 127 - 7, 1), 1, 254)
    codes = (b * np.exp2(127.0 - byte)[:, None, :]).reshape(r, m).astype(np.float32).astype(ml_dtypes.float8_e4m3fn).view(np.uint8)
    words = codes.reshape(r // 512, 128, 4, m).transpose(0, 1, 3, 2)
    return np.ascontiguousarray(words), np.ascontiguousarray(byte.astype(np.uint8).reshape(r // 512, 16, m))


D, T, I, Q, E = 512, 2048, 512, 256, 512


def setup_inputs():
    n = np.random.standard_normal
    idx = np.random.permutation(T)[:I]
    fd = mx_kscale(D)
    fi = mx_kscale(I)
    ti = np.ones(T)
    ti[idx] = fi
    keysp = pack_weight(n((D, T)) / fd[:, None], "e2m1")
    return {
        "query": (n((D, Q)) * 0.4 / np.sqrt(D) * fd[:, None]).astype(np.float32),
        "keys_words": keysp[0],
        "keys_scales": keysp[1],
        "fac": (np.random.uniform(0.5, 2.0, (I, 1)) * fi[:, None]).astype(np.float32),
        "vals": (n((E, T)) / ti).astype(np.float32),
        "offs": striped(idx),
    }


def reference(query, keys_words, keys_scales, fac, vals, offs):
    idx = unstriped(offs)
    keysu = unpack_weight(keys_words, keys_scales, "e2m1")
    queryq = mxq(f64(query), 0, "e4m3")
    keysidxg = keysu[:, idx]
    a = queryq.T @ keysidxg
    p = np.exp(a)
    r = p / np.sum(p, axis=1, keepdims=True)
    rt = r.T
    w = rt * f64(fac) / np.sum(rt, axis=1, keepdims=True)
    vt = f64(vals)[:, idx].T
    vtq = mxq(vt, 0, "e4m3")
    wq = mxq(w, 0, "e4m3")
    o = vtq.T @ wq
    words, scales = planes(o)
    return o, words, scales

@@ -1,0 +1,230 @@
+from contextlib import ExitStack
+
+import concourse.mybir as mybir
+from concourse.masks import make_identity
+
+D, T, I, Q, E = 512, 2048, 512, 256, 512
+FLOPS = 2 * Q * I * D + 2 * E * Q * I
+
+F32 = mybir.dt.float32
+BF16 = mybir.dt.bfloat16
+I32 = mybir.dt.int32
+U32 = mybir.dt.uint32
+U16 = mybir.dt.uint16
+U8 = mybir.dt.uint8
+FP8X4 = mybir.dt.float8_e4m3fn_x4
+FP4X4 = mybir.dt.float4_e2m1fn_x4
+ACT = mybir.ActivationFunctionType
+ALU = mybir.AluOpType
+AX = mybir.AxisListType
+
+P = 128
+PACK = 4
+HALVES = Q // P
+
+
+def tile_attend_sinkhorn_pl_kernel(tc, query, keys_words, keys_scales, fac, vals, offs, out_0, out_1, out_2):
+    nc = tc.nc
+    with ExitStack() as ctx:
+        sb = ctx.enter_context(tc.tile_pool(name="sb", bufs=1))
+        ps = ctx.enter_context(tc.psum_pool(name="ps", bufs=1))
+
+        offsets = sb.tile([P, I // 16], U16, name="offsets")
+        nc.sync.dma_start(offsets[:], offs)
+
+        key_scale_pool = sb.tile([P, T], U8, name="key_scale_pool")
+        for quad in range(4):
+            nc.sync.dma_start(
+                key_scale_pool[32 * quad : 32 * quad + 32, :].bitcast(I32),
+                keys_scales[0, 4 * quad : 4 * quad + 4, :].bitcast(I32).unsqueeze(0).to_broadcast([8, 4, T // 4]),
+            )
+        key_word_pool = sb.tile([P, T], U16, name="key_word_pool")
+        nc.sync.dma_start(key_word_pool[:].bitcast(I32), keys_words[0].bitcast(I32))
+        query_rows = []
+        for h in range(HALVES):
+            tile = sb.tile([P, PACK, P], F32, name=f"query_rows{h}")
+            nc.sync.dma_start(tile[:], query.rearrange("(p t) q -> p t q", t=PACK)[:, :, h * P : (h + 1) * P])
+            query_rows.append(tile)
+        fac_rows = sb.tile([P, PACK], F32, name="fac_rows")
+        nc.gpsimd.dma_start(fac_rows[:], fac.rearrange("(p t) o -> p (t o)", t=PACK))
+        val_planes = vals.rearrange("(p j) t -> j p t", j=PACK)
+        val_pool = []
+        for j in range(PACK):
+            plane = sb.tile([P, T], F32, name=f"val_pool{j}", tag=f"val_pool{j}", align_bytes=64)
+            nc.sync.dma_start(plane[:], val_planes[j])
+            val_pool.append(plane)
+
+        ident = sb.tile([P, P], F32, name="ident")
+        make_identity(nc, ident[:])
+
+        key_scales = sb.tile([P, I], U8, name="key_scales", align_bytes=64)
+        nc.vector.tensor_copy(key_scales[:], key_scale_pool[:].indirect(offsets[:]))
+        key_words = sb.tile([P, I], U16, name="key_words", align_bytes=64)
+        nc.vector.tensor_copy(key_words[:], key_word_pool[:].indirect(offsets[:]))
+        query_codes, query_scales = [], []
+        for h in range(HALVES):
+            grouped = sb.tile([P, P, PACK], BF16, name=f"query_grouped{h}", align_bytes=64)
+            nc.scalar.activation(
+                grouped[:].rearrange("p (c i) t -> p c t i", i=4),
+                query_rows[h][:].rearrange("p t (c i) -> p c t i", i=4),
+                ACT.Copy,
+            )
+            codes = sb.tile([P, P], U32, name=f"query_codes{h}", align_bytes=64)
+            scales = sb.tile([P, P], U8, name=f"query_scales{h}", align_bytes=64)
+            nc.vector.quantize_mx(codes[:].bitcast(FP8X4), scales[:], grouped[:].rearrange("p q t -> p (q t)"))
+            query_codes.append(codes)
+            query_scales.append(scales)
+
+        scores, neg_max = [], []
+        for h in range(HALVES):
+            bank = ps.tile([P, I], F32, name=f"scores{h}", tag=f"scores{h}")
+            nc.tensor.matmul_mx(
+                out=bank[:],
+                lhsT=query_codes[h][:].bitcast(FP8X4),
+                lhsT_scale=query_scales[h][:],
+                rhs=key_words[:].bitcast(FP4X4),
+                rhs_scale=key_scales[:],
+                start=True,
+                stop=True,
+            )
+            scores.append(bank)
+        for h in range(HALVES):
+            col = sb.tile([P, 1], F32, name=f"neg_max{h}", tag=f"neg_max{h}", align_bytes=64)
+            nc.vector.tensor_reduce(col[:], scores[h][:], AX.X, ALU.max, negate=True)
+            neg_max.append(col)
+
+        def gather_values(j, tag):
+            picked = sb.tile([P, I], BF16, name=f"val_picked{j}", tag=tag, align_bytes=64)
+            nc.vector.tensor_copy(picked[:], val_pool[j][:].indirect(offsets[:]))
+            return picked
+
+        def turn_values(picked, bank_tag, grouped):
+            turned = ps.tile([P, 2, P], F32, name="val_turned", tag=bank_tag)
+            pairs = picked[:].bitcast(F32)
+            for u in range(2):
+                nc.tensor.transpose(turned[:, u, :], pairs[:, u : I // 2 : 2], ident[:])
+            nc.scalar.copy(
+                grouped.bitcast(F32).rearrange("p (e u) -> p e u", u=2),
+                turned[:].rearrange("p u e -> p e u"),
+            )
+
+        def quantize(grouped, width, name, tag):
+            codes = sb.tile([P, width], U32, name=f"{name}_codes", tag=tag, align_bytes=64)
+            scales = sb.tile([P, width], U8, name=f"{name}_scales", align_bytes=64)
+            nc.vector.quantize_mx(codes[:].bitcast(FP8X4), scales[:], grouped)
+            return codes, scales
+
+        expd, row_sum = [], []
+        for h in range(HALVES):
+            tile = sb.tile([P, PACK, P], F32, name=f"expd{h}", tag=f"expd{h}", align_bytes=64)
+            col = sb.tile([P, 1], F32, name=f"row_sum{h}", tag=f"row_sum{h}", align_bytes=64)
+            nc.scalar.activation(
+                tile[:],
+                scores[h][:].rearrange("p (s t) -> p t s", t=PACK),
+                ACT.Exp,
+                bias=neg_max[h][:],
+                accum_out=col[:],
+            )
+            expd.append(tile)
+            row_sum.append(col)
+        rows = []
+        for h in range(HALVES):
+            inv = sb.tile([P, 1], F32, name=f"row_inv{h}")
+            nc.vector.reciprocal(inv[:], row_sum[h][:])
+            tile = sb.tile([P, PACK, P], F32, name=f"rows{h}")
+            nc.vector.tensor_scalar(tile[:], expd[h][:], inv[:], None, ALU.mult)
+            rows.append(tile)
+        picked0 = gather_values(0, "row_sum1")
+        picked1 = gather_values(1, "expd1")
+
+        slots = []
+        for h in range(HALVES):
+            bank = ps.tile([P, PACK, P], F32, name=f"slots{h}", tag=f"slots{h}")
+            for t in range(PACK):
+                nc.tensor.transpose(bank[:, t, :], rows[h][:, t, :], ident[:])
+            slots.append(bank)
+        part_sum = sb.tile([P, PACK], F32, name="part_sum")
+        slot_sum = sb.tile([P, PACK], F32, name="slot_sum", tag="slot_sum", align_bytes=64)
+        spent = sb.tile([P, PACK, P], F32, name="spent", tag="spent", align_bytes=64)
+        for t in range(PACK):
+            nc.scalar.activation(
+                spent[:, t, :], slots[0][:, t, :], ACT.Copy, scale=1.0 / P, accum_out=part_sum[:, t : t + 1]
+            )
+        for t in range(PACK):
+            nc.scalar.activation(
+                spent[:, t, :], slots[1][:, t, :], ACT.Identity,
+                bias=part_sum[:, t : t + 1], accum_out=slot_sum[:, t : t + 1],
+            )
+        slot_inv = sb.tile([P, PACK], F32, name="slot_inv", tag="slot_inv", align_bytes=64)
+        nc.vector.reciprocal(slot_inv[:], slot_sum[:])
+        picked2 = gather_values(2, "spent")
+        slot_gain = sb.tile([P, PACK], F32, name="slot_gain", tag="slot_gain", align_bytes=64)
+        nc.vector.tensor_tensor(slot_gain[:], slot_inv[:], fac_rows[:], ALU.mult)
+
+        def weigh(h):
+            grouped = sb.tile([P, P, PACK], BF16, name=f"weight_grouped{h}", align_bytes=64)
+            nc.vector.tensor_tensor(
+                grouped[:],
+                slots[h][:].rearrange("p t q -> p q t"),
+                slot_gain[:].unsqueeze(1).to_broadcast([P, P, PACK]),
+                ALU.mult,
+            )
+            return grouped[:].rearrange("p q t -> p (q t)")
+
+        result = [ps.tile([P, PACK, P], F32, name=f"result{h}") for h in range(HALVES)]
+
+        def multiply(j, h, val, weight):
+            nc.tensor.matmul_mx(
+                out=result[h][:, j, :],
+                lhsT=val[0].bitcast(FP8X4),
+                lhsT_scale=val[1],
+                rhs=weight[0][:].bitcast(FP8X4),
+                rhs_scale=weight[1][:],
+                start=True,
+                stop=True,
+            )
+
+        grouped01 = sb.tile([P, 2 * I], BF16, name="grouped01", tag="grouped01", align_bytes=64)
+        turn_values(picked0, "turned", grouped01[:, 0:I])
+        turn_values(picked1, "scores0", grouped01[:, I : 2 * I])
+        codes01, scales01 = quantize(grouped01[:], 2 * P, "val01", "slot_sum")
+        val_mx = [(codes01[:, a * P : (a + 1) * P], scales01[:, a * P : (a + 1) * P]) for a in range(2)]
+        grouped2 = sb.tile([P, I], BF16, name="grouped2", align_bytes=64)
+        turn_values(picked2, "scores1", grouped2[:])
+        weighed0 = weigh(0)
+        picked3 = gather_values(3, "slot_inv")
+        grouped3 = sb.tile([P, I], BF16, name="grouped3", align_bytes=64)
+        turn_values(picked3, "turned", grouped3[:])
+        weighed1 = weigh(1)
+        weight0 = quantize(weighed0, P, "weight0", "weight0")
+        codes2, scales2 = quantize(grouped2[:], P, "val2", "grouped01")
+        val_mx.append((codes2[:], scales2[:]))
+        for j in range(3):
+            multiply(j, 0, val_mx[j], weight0)
+        weight1 = quantize(weighed1, P, "weight1", "weight1")
+        for j in range(3):
+            multiply(j, 1, val_mx[j], weight1)
+        codes3, scales3 = quantize(grouped3[:], P, "val3", "val3")
+        for h, weight in enumerate((weight0, weight1)):
+            multiply(3, h, (codes3[:], scales3[:]), weight)
+
+        out_rows = out_0.rearrange("(p j) q -> p j q", j=PACK)
+        rounded = sb.tile([P, Q, PACK], BF16, name="rounded", align_bytes=64)
+        staged = [sb.tile([P, PACK, P], F32, name=f"staged{h}") for h in range(HALVES)]
+        nc.vector.tensor_copy(rounded[:, 0:P, :], result[0][:].rearrange("p j q -> p q j"))
+        nc.scalar.copy(staged[1][:], result[1][:])
+        nc.sync.dma_start(out_rows[:, :, P:Q], staged[1][:])
+        nc.vector.tensor_copy(
+            rounded[:, P:Q, :].rearrange("p (c i) j -> p c j i", i=4),
+            staged[1][:].rearrange("p j (c i) -> p c j i", i=4),
+        )
+        nc.scalar.copy(staged[0][:], result[0][:])
+        nc.sync.dma_start(out_rows[:, :, 0:P], staged[0][:])
+        out_codes, out_scales = quantize(rounded[:].rearrange("p q j -> p (q j)"), Q, "out", "out_codes")
+        nc.sync.dma_start(out_1[0].rearrange("p c t -> p (c t)").bitcast(I32), out_codes[:].bitcast(I32))
+        for quad in range(4):
+            queue = nc.sync if quad % 2 else nc.scalar
+            queue.dma_start(
+                out_2[0, 4 * quad : 4 * quad + 4, :].bitcast(I32),
+                out_scales[32 * quad : 32 * quad + 4, :].bitcast(I32),
+            )

@@ -27,6 +27,7 @@ def tile_attend_sinkhorn_pl_kernel(tc, query, keys_words, keys_scales, fac, vals
     nc = tc.nc
     with ExitStack() as ctx:
         sb = ctx.enter_context(tc.tile_pool(name="sb", bufs=1))
+        late = ctx.enter_context(tc.tile_pool(name="late", bufs=1))
         ps = ctx.enter_context(tc.psum_pool(name="ps", bufs=1))
 
         offsets = sb.tile([P, I // 16], U16, name="offsets")
@@ -50,7 +51,10 @@ def tile_attend_sinkhorn_pl_kernel(tc, query, keys_words, keys_scales, fac, vals
         val_planes = vals.rearrange("(p j) t -> j p t", j=PACK)
         val_pool = []
         for j in range(PACK):
-            plane = sb.tile([P, T], F32, name=f"val_pool{j}", tag=f"val_pool{j}", align_bytes=64)
+            if j == PACK - 1:
+                plane = late.tile([P, T], F32, name=f"val_pool{j}", offset=0, align_bytes=64)
+            else:
+                plane = sb.tile([P, T], F32, name=f"val_pool{j}", tag=f"val_pool{j}", align_bytes=64)
             nc.sync.dma_start(plane[:], val_planes[j])
             val_pool.append(plane)
 
@@ -69,7 +73,7 @@ def tile_attend_sinkhorn_pl_kernel(tc, query, keys_words, keys_scales, fac, vals
                 query_rows[h][:].rearrange("p t (c i) -> p c t i", i=4),
                 ACT.Copy,
             )
-            codes = sb.tile([P, P], U32, name=f"query_codes{h}", align_bytes=64)
+            codes = sb.tile([P, P], U32, name=f"query_codes{h}", tag=f"query_codes{h}", align_bytes=64)
             scales = sb.tile([P, P], U8, name=f"query_scales{h}", align_bytes=64)
             nc.vector.quantize_mx(codes[:].bitcast(FP8X4), scales[:], grouped[:].rearrange("p q t -> p (q t)"))
             query_codes.append(codes)
@@ -108,12 +112,16 @@ def tile_attend_sinkhorn_pl_kernel(tc, query, keys_words, keys_scales, fac, vals
                 turned[:].rearrange("p u e -> p e u"),
             )
 
-        def quantize(grouped, width, name, tag):
-            codes = sb.tile([P, width], U32, name=f"{name}_codes", tag=tag, align_bytes=64)
+        def quantize(grouped, width, name, tag, offset=None):
+            if offset is None:
+                codes = sb.tile([P, width], U32, name=f"{name}_codes", tag=tag, align_bytes=64)
+            else:
+                codes = late.tile([P, width], U32, name=f"{name}_codes", offset=offset, align_bytes=64)
             scales = sb.tile([P, width], U8, name=f"{name}_scales", align_bytes=64)
             nc.vector.quantize_mx(codes[:].bitcast(FP8X4), scales[:], grouped)
             return codes, scales
 
+        picked0 = gather_values(0, "query_codes1")
         expd, row_sum = [], []
         for h in range(HALVES):
             tile = sb.tile([P, PACK, P], F32, name=f"expd{h}", tag=f"expd{h}", align_bytes=64)
@@ -127,15 +135,17 @@ def tile_attend_sinkhorn_pl_kernel(tc, query, keys_words, keys_scales, fac, vals
             )
             expd.append(tile)
             row_sum.append(col)
-        rows = []
+        row_inv, rows = [], []
         for h in range(HALVES):
             inv = sb.tile([P, 1], F32, name=f"row_inv{h}")
             nc.vector.reciprocal(inv[:], row_sum[h][:])
-            tile = sb.tile([P, PACK, P], F32, name=f"rows{h}")
-            nc.vector.tensor_scalar(tile[:], expd[h][:], inv[:], None, ALU.mult)
+            row_inv.append(inv)
+        for h, tag in enumerate(("neg_max1", "rows1")):
+            tile = sb.tile([P, PACK, P], F32, name=f"rows{h}", tag=tag, align_bytes=64)
+            nc.vector.tensor_scalar(tile[:], expd[h][:], row_inv[h][:], None, ALU.mult)
             rows.append(tile)
-        picked0 = gather_values(0, "row_sum1")
-        picked1 = gather_values(1, "expd1")
+        picked1 = gather_values(1, "expd0")
+        picked2 = gather_values(2, "expd1")
 
         slots = []
         for h in range(HALVES):
@@ -157,17 +167,18 @@ def tile_attend_sinkhorn_pl_kernel(tc, query, keys_words, keys_scales, fac, vals
             )
         slot_inv = sb.tile([P, PACK], F32, name="slot_inv", tag="slot_inv", align_bytes=64)
         nc.vector.reciprocal(slot_inv[:], slot_sum[:])
-        picked2 = gather_values(2, "spent")
-        slot_gain = sb.tile([P, PACK], F32, name="slot_gain", tag="slot_gain", align_bytes=64)
-        nc.vector.tensor_tensor(slot_gain[:], slot_inv[:], fac_rows[:], ALU.mult)
 
         def weigh(h):
-            grouped = sb.tile([P, P, PACK], BF16, name=f"weight_grouped{h}", align_bytes=64)
-            nc.vector.tensor_tensor(
-                grouped[:],
-                slots[h][:].rearrange("p t q -> p q t"),
-                slot_gain[:].unsqueeze(1).to_broadcast([P, P, PACK]),
-                ALU.mult,
+            planes = sb.tile([P, PACK, P], BF16, name=f"weight_planes{h}")
+            for t in range(PACK):
+                nc.scalar.activation(planes[:, t, :], slots[h][:, t, :], ACT.Copy, scale=slot_gain[:, t : t + 1])
+            return planes
+
+        def interleave(h, planes):
+            grouped = late.tile([P, P, PACK], BF16, name=f"weight_grouped{h}", offset=1024 * h, align_bytes=64)
+            nc.vector.tensor_copy(
+                grouped[:].rearrange("p (c i) t -> p c t i", i=4),
+                planes[:].rearrange("p t (c i) -> p c t i", i=4),
             )
             return grouped[:].rearrange("p q t -> p (q t)")
 
@@ -187,44 +198,46 @@ def tile_attend_sinkhorn_pl_kernel(tc, query, keys_words, keys_scales, fac, vals
         grouped01 = sb.tile([P, 2 * I], BF16, name="grouped01", tag="grouped01", align_bytes=64)
         turn_values(picked0, "turned", grouped01[:, 0:I])
         turn_values(picked1, "scores0", grouped01[:, I : 2 * I])
-        codes01, scales01 = quantize(grouped01[:], 2 * P, "val01", "slot_sum")
+        codes01, scales01 = quantize(grouped01[:], 2 * P, "val01", "spent")
         val_mx = [(codes01[:, a * P : (a + 1) * P], scales01[:, a * P : (a + 1) * P]) for a in range(2)]
+        slot_gain = sb.tile([P, PACK], F32, name="slot_gain", tag="slot_gain", align_bytes=64)
+        nc.vector.tensor_tensor(slot_gain[:], slot_inv[:], fac_rows[:], ALU.mult)
+
+        planes = [weigh(h) for h in range(HALVES)]
         grouped2 = sb.tile([P, I], BF16, name="grouped2", align_bytes=64)
         turn_values(picked2, "scores1", grouped2[:])
-        weighed0 = weigh(0)
-        picked3 = gather_values(3, "slot_inv")
+        picked3 = gather_values(3, "slot_sum")
         grouped3 = sb.tile([P, I], BF16, name="grouped3", align_bytes=64)
         turn_values(picked3, "turned", grouped3[:])
-        weighed1 = weigh(1)
+        weighed0 = interleave(0, planes[0])
+        codes, scales = quantize(grouped2[:], P, "val2", None, 2048)
+        val_mx.append((codes[:], scales[:]))
         weight0 = quantize(weighed0, P, "weight0", "weight0")
-        codes2, scales2 = quantize(grouped2[:], P, "val2", "grouped01")
-        val_mx.append((codes2[:], scales2[:]))
-        for j in range(3):
-            multiply(j, 0, val_mx[j], weight0)
+        weighed1 = interleave(1, planes[1])
+        codes, scales = quantize(grouped3[:], P, "val3", "val3")
+        val_mx.append((codes[:], scales[:]))
         weight1 = quantize(weighed1, P, "weight1", "weight1")
-        for j in range(3):
-            multiply(j, 1, val_mx[j], weight1)
-        codes3, scales3 = quantize(grouped3[:], P, "val3", "val3")
-        for h, weight in enumerate((weight0, weight1)):
-            multiply(3, h, (codes3[:], scales3[:]), weight)
 
         out_rows = out_0.rearrange("(p j) q -> p j q", j=PACK)
         rounded = sb.tile([P, Q, PACK], BF16, name="rounded", align_bytes=64)
-        staged = [sb.tile([P, PACK, P], F32, name=f"staged{h}") for h in range(HALVES)]
-        nc.vector.tensor_copy(rounded[:, 0:P, :], result[0][:].rearrange("p j q -> p q j"))
-        nc.scalar.copy(staged[1][:], result[1][:])
-        nc.sync.dma_start(out_rows[:, :, P:Q], staged[1][:])
-        nc.vector.tensor_copy(
-            rounded[:, P:Q, :].rearrange("p (c i) j -> p c j i", i=4),
-            staged[1][:].rearrange("p j (c i) -> p c j i", i=4),
-        )
-        nc.scalar.copy(staged[0][:], result[0][:])
-        nc.sync.dma_start(out_rows[:, :, 0:P], staged[0][:])
-        out_codes, out_scales = quantize(rounded[:].rearrange("p q j -> p (q j)"), Q, "out", "out_codes")
+        out_codes = sb.tile([P, Q], U32, name="out_codes", align_bytes=64)
+        out_scales = sb.tile([P, Q], U8, name="out_scales", align_bytes=64)
+        for h, weight in enumerate((weight0, weight1)):
+            cols = slice(h * P, (h + 1) * P)
+            for j in range(PACK):
+                multiply(j, h, val_mx[j], weight)
+            nc.vector.tensor_copy(rounded[:, cols, :], result[h][:].rearrange("p j q -> p q j"))
+            staged = sb.tile([P, PACK, P], F32, name=f"staged{h}")
+            nc.scalar.copy(staged[:], result[h][:])
+            nc.scalar.dma_start(out_rows[:, :, cols], staged[:])
+        for h in range(HALVES):
+            cols = slice(h * P, (h + 1) * P)
+            nc.vector.quantize_mx(
+                out_codes[:, cols].bitcast(FP8X4), out_scales[:, cols], rounded[:, cols, :].rearrange("p q j -> p (q j)")
+            )
         nc.sync.dma_start(out_1[0].rearrange("p c t -> p (c t)").bitcast(I32), out_codes[:].bitcast(I32))
         for quad in range(4):
-            queue = nc.sync if quad % 2 else nc.scalar
-            queue.dma_start(
+            nc.sync.dma_start(
                 out_2[0, 4 * quad : 4 * quad + 4, :].bitcast(I32),
                 out_scales[32 * quad : 32 * quad + 4, :].bitcast(I32),
             )

@@ -21,71 +21,76 @@ AX = mybir.AxisListType
 P = 128
 PACK = 4
 HALVES = Q // P
+LAST = PACK - 1
+SPLIT = 160
 
 
 def tile_attend_sinkhorn_pl_kernel(tc, query, keys_words, keys_scales, fac, vals, offs, out_0, out_1, out_2):
     nc = tc.nc
     with ExitStack() as ctx:
         sb = ctx.enter_context(tc.tile_pool(name="sb", bufs=1))
-        late = ctx.enter_context(tc.tile_pool(name="late", bufs=1))
+        after2 = ctx.enter_context(tc.tile_pool(name="after2", bufs=1))
+        after3 = ctx.enter_context(tc.tile_pool(name="after3", bufs=1))
         ps = ctx.enter_context(tc.psum_pool(name="ps", bufs=1))
 
         offsets = sb.tile([P, I // 16], U16, name="offsets")
         nc.sync.dma_start(offsets[:], offs)
-
-        key_scale_pool = sb.tile([P, T], U8, name="key_scale_pool")
-        for quad in range(4):
-            nc.sync.dma_start(
-                key_scale_pool[32 * quad : 32 * quad + 32, :].bitcast(I32),
-                keys_scales[0, 4 * quad : 4 * quad + 4, :].bitcast(I32).unsqueeze(0).to_broadcast([8, 4, T // 4]),
-            )
         key_word_pool = sb.tile([P, T], U16, name="key_word_pool")
         nc.sync.dma_start(key_word_pool[:].bitcast(I32), keys_words[0].bitcast(I32))
-        query_rows = []
-        for h in range(HALVES):
-            tile = sb.tile([P, PACK, P], F32, name=f"query_rows{h}")
-            nc.sync.dma_start(tile[:], query.rearrange("(p t) q -> p t q", t=PACK)[:, :, h * P : (h + 1) * P])
-            query_rows.append(tile)
         fac_rows = sb.tile([P, PACK], F32, name="fac_rows")
-        nc.gpsimd.dma_start(fac_rows[:], fac.rearrange("(p t) o -> p (t o)", t=PACK))
+        nc.scalar.dma_start(fac_rows[:], fac.rearrange("(p t) o -> p (t o)", t=PACK))
+
+        key_scale_pool = sb.tile([P, T], U8, name="key_scale_pool")
+        nc.gpsimd.memset(key_scale_pool[:].bitcast(I32), 0)
+        scale_rows = keys_scales[0].bitcast(I32).rearrange("(quad r) c -> r quad c", r=4)
+        for r in range(4):
+            nc.sync.dma_start(key_scale_pool[r:P:32, :].bitcast(I32), scale_rows[r])
+        query_rows = sb.tile([P, PACK, Q], F32, name="query_rows")
+        nc.sync.dma_start(query_rows[:], query.rearrange("(p t) q -> p t q", t=PACK))
         val_planes = vals.rearrange("(p j) t -> j p t", j=PACK)
         val_pool = []
-        for j in range(PACK):
-            if j == PACK - 1:
-                plane = late.tile([P, T], F32, name=f"val_pool{j}", offset=0, align_bytes=64)
+        for j, pool in enumerate((sb, sb, after2, after3)):
+            if pool is sb:
+                plane = pool.tile([P, T], F32, name=f"val_pool{j}", align_bytes=64)
             else:
-                plane = sb.tile([P, T], F32, name=f"val_pool{j}", tag=f"val_pool{j}", align_bytes=64)
+                plane = pool.tile([P, T], F32, name=f"val_pool{j}", offset=0, align_bytes=64)
             nc.sync.dma_start(plane[:], val_planes[j])
             val_pool.append(plane)
 
         ident = sb.tile([P, P], F32, name="ident")
         make_identity(nc, ident[:])
 
-        key_scales = sb.tile([P, I], U8, name="key_scales", align_bytes=64)
-        nc.vector.tensor_copy(key_scales[:], key_scale_pool[:].indirect(offsets[:]))
+        def quantize(grouped, width, name, offset=None):
+            if offset is None:
+                codes = sb.tile([P, width], U32, name=f"{name}_codes", align_bytes=64)
+            else:
+                codes = after3.tile([P, width], U32, name=f"{name}_codes", offset=offset, align_bytes=64)
+            scales = sb.tile([P, width], U8, name=f"{name}_scales", align_bytes=64)
+            nc.vector.quantize_mx(codes[:].bitcast(FP8X4), scales[:], grouped)
+            return [(codes[:, a : a + P], scales[:, a : a + P]) for a in range(0, width, P)]
+
         key_words = sb.tile([P, I], U16, name="key_words", align_bytes=64)
         nc.vector.tensor_copy(key_words[:], key_word_pool[:].indirect(offsets[:]))
-        query_codes, query_scales = [], []
+        key_scales = sb.tile([P, I], U8, name="key_scales", align_bytes=64)
+        nc.vector.tensor_copy(key_scales[:], key_scale_pool[:].indirect(offsets[:]))
+        query_grouped = []
         for h in range(HALVES):
             grouped = sb.tile([P, P, PACK], BF16, name=f"query_grouped{h}", align_bytes=64)
-            nc.scalar.activation(
-                grouped[:].rearrange("p (c i) t -> p c t i", i=4),
-                query_rows[h][:].rearrange("p t (c i) -> p c t i", i=4),
-                ACT.Copy,
-            )
-            codes = sb.tile([P, P], U32, name=f"query_codes{h}", tag=f"query_codes{h}", align_bytes=64)
-            scales = sb.tile([P, P], U8, name=f"query_scales{h}", align_bytes=64)
-            nc.vector.quantize_mx(codes[:].bitcast(FP8X4), scales[:], grouped[:].rearrange("p q t -> p (q t)"))
-            query_codes.append(codes)
-            query_scales.append(scales)
+            dst = grouped[:].rearrange("p (c i) t -> p c t i", i=4)
+            src = query_rows[:, :, h * P : (h + 1) * P].rearrange("p t (c i) -> p c t i", i=4)
+            nc.scalar.activation(dst, src, ACT.Copy)
+            query_grouped.append(grouped)
+        query_mx = [
+            quantize(query_grouped[h][:].rearrange("p q t -> p (q t)"), P, f"query{h}")[0] for h in range(HALVES)
+        ]
 
         scores, neg_max = [], []
         for h in range(HALVES):
             bank = ps.tile([P, I], F32, name=f"scores{h}", tag=f"scores{h}")
             nc.tensor.matmul_mx(
                 out=bank[:],
-                lhsT=query_codes[h][:].bitcast(FP8X4),
-                lhsT_scale=query_scales[h][:],
+                lhsT=query_mx[h][0].bitcast(FP8X4),
+                lhsT_scale=query_mx[h][1],
                 rhs=key_words[:].bitcast(FP4X4),
                 rhs_scale=key_scales[:],
                 start=True,
@@ -97,35 +102,10 @@ def tile_attend_sinkhorn_pl_kernel(tc, query, keys_words, keys_scales, fac, vals
             nc.vector.tensor_reduce(col[:], scores[h][:], AX.X, ALU.max, negate=True)
             neg_max.append(col)
 
-        def gather_values(j, tag):
-            picked = sb.tile([P, I], BF16, name=f"val_picked{j}", tag=tag, align_bytes=64)
-            nc.vector.tensor_copy(picked[:], val_pool[j][:].indirect(offsets[:]))
-            return picked
-
-        def turn_values(picked, bank_tag, grouped):
-            turned = ps.tile([P, 2, P], F32, name="val_turned", tag=bank_tag)
-            pairs = picked[:].bitcast(F32)
-            for u in range(2):
-                nc.tensor.transpose(turned[:, u, :], pairs[:, u : I // 2 : 2], ident[:])
-            nc.scalar.copy(
-                grouped.bitcast(F32).rearrange("p (e u) -> p e u", u=2),
-                turned[:].rearrange("p u e -> p e u"),
-            )
-
-        def quantize(grouped, width, name, tag, offset=None):
-            if offset is None:
-                codes = sb.tile([P, width], U32, name=f"{name}_codes", tag=tag, align_bytes=64)
-            else:
-                codes = late.tile([P, width], U32, name=f"{name}_codes", offset=offset, align_bytes=64)
-            scales = sb.tile([P, width], U8, name=f"{name}_scales", align_bytes=64)
-            nc.vector.quantize_mx(codes[:].bitcast(FP8X4), scales[:], grouped)
-            return codes, scales
-
-        picked0 = gather_values(0, "query_codes1")
         expd, row_sum = [], []
         for h in range(HALVES):
-            tile = sb.tile([P, PACK, P], F32, name=f"expd{h}", tag=f"expd{h}", align_bytes=64)
-            col = sb.tile([P, 1], F32, name=f"row_sum{h}", tag=f"row_sum{h}", align_bytes=64)
+            tile = sb.tile([P, PACK, P], F32, name=f"expd{h}", align_bytes=64)
+            col = sb.tile([P, 1], F32, name=f"row_sum{h}", align_bytes=64)
             nc.scalar.activation(
                 tile[:],
                 scores[h][:].rearrange("p (s t) -> p t s", t=PACK),
@@ -135,101 +115,120 @@ def tile_attend_sinkhorn_pl_kernel(tc, query, keys_words, keys_scales, fac, vals
             )
             expd.append(tile)
             row_sum.append(col)
-        row_inv, rows = [], []
+        slots = []
         for h in range(HALVES):
             inv = sb.tile([P, 1], F32, name=f"row_inv{h}")
             nc.vector.reciprocal(inv[:], row_sum[h][:])
-            row_inv.append(inv)
-        for h, tag in enumerate(("neg_max1", "rows1")):
-            tile = sb.tile([P, PACK, P], F32, name=f"rows{h}", tag=tag, align_bytes=64)
-            nc.vector.tensor_scalar(tile[:], expd[h][:], row_inv[h][:], None, ALU.mult)
-            rows.append(tile)
-        picked1 = gather_values(1, "expd0")
-        picked2 = gather_values(2, "expd1")
-
-        slots = []
-        for h in range(HALVES):
-            bank = ps.tile([P, PACK, P], F32, name=f"slots{h}", tag=f"slots{h}")
+            tile = sb.tile([P, PACK, P], F32, name=f"rows{h}", align_bytes=64)
+            nc.vector.tensor_scalar(tile[:], expd[h][:], inv[:], None, ALU.mult)
+            bank = ps.tile([P, PACK, P], F32, name=f"slots{h}")
             for t in range(PACK):
-                nc.tensor.transpose(bank[:, t, :], rows[h][:, t, :], ident[:])
+                nc.tensor.transpose(bank[:, t, :], tile[:, t, :], ident[:])
             slots.append(bank)
-        part_sum = sb.tile([P, PACK], F32, name="part_sum")
-        slot_sum = sb.tile([P, PACK], F32, name="slot_sum", tag="slot_sum", align_bytes=64)
-        spent = sb.tile([P, PACK, P], F32, name="spent", tag="spent", align_bytes=64)
-        for t in range(PACK):
-            nc.scalar.activation(
-                spent[:, t, :], slots[0][:, t, :], ACT.Copy, scale=1.0 / P, accum_out=part_sum[:, t : t + 1]
+
+        def turn(picked, turned):
+            pairs = picked.bitcast(F32)
+            for u in range(2):
+                nc.tensor.transpose(turned[:, u, :], pairs[:, u : I // 2 : 2], ident[:])
+
+        def group(grouped, turned):
+            nc.scalar.copy(
+                grouped.bitcast(F32).rearrange("p (j e u) -> p j e u", u=2, e=P),
+                turned.rearrange("p (j u) e -> p j e u", u=2),
             )
-        for t in range(PACK):
-            nc.scalar.activation(
-                spent[:, t, :], slots[1][:, t, :], ACT.Identity,
-                bias=part_sum[:, t : t + 1], accum_out=slot_sum[:, t : t + 1],
-            )
-        slot_inv = sb.tile([P, PACK], F32, name="slot_inv", tag="slot_inv", align_bytes=64)
+
+        picked01 = sb.tile([P, 2, I], BF16, name="picked01", align_bytes=64)
+        for j in range(2):
+            nc.scalar.activation(picked01[:, j, :], val_pool[j][:].indirect(offsets[:]), ACT.Copy)
+        picked2 = sb.tile([P, I], BF16, name="picked2", align_bytes=64)
+        nc.scalar.activation(picked2[:], val_pool[2][:].indirect(offsets[:]), ACT.Copy)
+
+        part_sum = sb.tile([P, HALVES, PACK], F32, name="part_sum")
+        for h in range(HALVES):
+            nc.vector.tensor_reduce(part_sum[:, h, :], slots[h][:], AX.X, ALU.add)
+        slot_sum = sb.tile([P, PACK], F32, name="slot_sum")
+        nc.vector.tensor_tensor(slot_sum[:], part_sum[:, 0, :], part_sum[:, 1, :], ALU.add)
+        slot_inv = sb.tile([P, PACK], F32, name="slot_inv")
         nc.vector.reciprocal(slot_inv[:], slot_sum[:])
-
-        def weigh(h):
-            planes = sb.tile([P, PACK, P], BF16, name=f"weight_planes{h}")
-            for t in range(PACK):
-                nc.scalar.activation(planes[:, t, :], slots[h][:, t, :], ACT.Copy, scale=slot_gain[:, t : t + 1])
-            return planes
-
-        def interleave(h, planes):
-            grouped = late.tile([P, P, PACK], BF16, name=f"weight_grouped{h}", offset=1024 * h, align_bytes=64)
-            nc.vector.tensor_copy(
-                grouped[:].rearrange("p (c i) t -> p c t i", i=4),
-                planes[:].rearrange("p t (c i) -> p c t i", i=4),
+        slot_gain = sb.tile([P, PACK], F32, name="slot_gain")
+        nc.vector.tensor_tensor(slot_gain[:], slot_inv[:], fac_rows[:], ALU.mult)
+        weighed = []
+        for h in range(HALVES):
+            grouped = sb.tile([P, P, PACK], BF16, name=f"weight_grouped{h}", align_bytes=64)
+            nc.vector.tensor_tensor(
+                grouped[:],
+                slots[h][:].rearrange("p t q -> p q t"),
+                slot_gain[:].unsqueeze(1).to_broadcast([P, P, PACK]),
+                ALU.mult,
             )
-            return grouped[:].rearrange("p q t -> p (q t)")
+            weighed.append(grouped)
 
-        result = [ps.tile([P, PACK, P], F32, name=f"result{h}") for h in range(HALVES)]
+        turned01 = ps.tile([P, 4, P], F32, name="turned01", tag="scores1")
+        for j in range(2):
+            turn(picked01[:, j, :], turned01[:, 2 * j : 2 * j + 2, :])
+        grouped01 = after2.tile([P, 2 * I], BF16, name="grouped01", offset=0, align_bytes=64)
+        group(grouped01[:], turned01[:])
+        turned2 = ps.tile([P, 2, P], F32, name="turned2", tag="scores0")
+        turn(picked2[:], turned2[:])
 
-        def multiply(j, h, val, weight):
+        picked3 = sb.tile([P, I], BF16, name="picked3", align_bytes=64)
+        nc.vector.tensor_copy(picked3[:, :SPLIT], val_pool[LAST][:].indirect(offsets[:, : SPLIT // 16]))
+        nc.scalar.activation(picked3[:, SPLIT:], val_pool[LAST][:].indirect(offsets[:, SPLIT // 16 :]), ACT.Copy)
+        turned3 = ps.tile([P, 2, P], F32, name="turned3", tag="scores1")
+        turn(picked3[:], turned3[:])
+        grouped2 = after3.tile([P, I], BF16, name="grouped2", offset=0, align_bytes=64)
+        group(grouped2[:], turned2[:])
+        weight_mx = quantize(weighed[0][:].rearrange("p q t -> p (q t)"), P, "weight0", 1024)
+        val_mx = quantize(grouped01[:], 2 * P, "val01", 2048)
+        weight_mx += quantize(weighed[1][:].rearrange("p q t -> p (q t)"), P, "weight1", 1536)
+        val_mx += quantize(grouped2[:], P, "val2")
+
+        result = [
+            [ps.tile([P, 2, P], F32, name=f"result{pair}{h}") for h in range(HALVES)] for pair in range(2)
+        ]
+
+        def multiply(j, h):
             nc.tensor.matmul_mx(
-                out=result[h][:, j, :],
-                lhsT=val[0].bitcast(FP8X4),
-                lhsT_scale=val[1],
-                rhs=weight[0][:].bitcast(FP8X4),
-                rhs_scale=weight[1][:],
+                out=result[j // 2][h][:, j % 2, :],
+                lhsT=val_mx[j][0].bitcast(FP8X4),
+                lhsT_scale=val_mx[j][1],
+                rhs=weight_mx[h][0].bitcast(FP8X4),
+                rhs_scale=weight_mx[h][1],
                 start=True,
                 stop=True,
             )
 
-        grouped01 = sb.tile([P, 2 * I], BF16, name="grouped01", tag="grouped01", align_bytes=64)
-        turn_values(picked0, "turned", grouped01[:, 0:I])
-        turn_values(picked1, "scores0", grouped01[:, I : 2 * I])
-        codes01, scales01 = quantize(grouped01[:], 2 * P, "val01", "spent")
-        val_mx = [(codes01[:, a * P : (a + 1) * P], scales01[:, a * P : (a + 1) * P]) for a in range(2)]
-        slot_gain = sb.tile([P, PACK], F32, name="slot_gain", tag="slot_gain", align_bytes=64)
-        nc.vector.tensor_tensor(slot_gain[:], slot_inv[:], fac_rows[:], ALU.mult)
-
-        planes = [weigh(h) for h in range(HALVES)]
-        grouped2 = sb.tile([P, I], BF16, name="grouped2", align_bytes=64)
-        turn_values(picked2, "scores1", grouped2[:])
-        picked3 = gather_values(3, "slot_sum")
+        for h in range(HALVES):
+            for j in range(2):
+                multiply(j, h)
+        for h in range(HALVES):
+            multiply(2, h)
         grouped3 = sb.tile([P, I], BF16, name="grouped3", align_bytes=64)
-        turn_values(picked3, "turned", grouped3[:])
-        weighed0 = interleave(0, planes[0])
-        codes, scales = quantize(grouped2[:], P, "val2", None, 2048)
-        val_mx.append((codes[:], scales[:]))
-        weight0 = quantize(weighed0, P, "weight0", "weight0")
-        weighed1 = interleave(1, planes[1])
-        codes, scales = quantize(grouped3[:], P, "val3", "val3")
-        val_mx.append((codes[:], scales[:]))
-        weight1 = quantize(weighed1, P, "weight1", "weight1")
-
+        group(grouped3[:], turned3[:])
+        val_mx += quantize(grouped3[:], P, "val3")
         out_rows = out_0.rearrange("(p j) q -> p j q", j=PACK)
         rounded = sb.tile([P, Q, PACK], BF16, name="rounded", align_bytes=64)
+        staged = [sb.tile([P, 2, Q], F32, name=f"staged{pair}") for pair in range(2)]
+
+        def stage(pair, h):
+            nc.scalar.copy(staged[pair][:, :, h * P : (h + 1) * P], result[pair][h][:])
+
+        def round_pair(copy, pair, h):
+            copy(rounded[:, h * P : (h + 1) * P, 2 * pair : 2 * pair + 2], result[pair][h][:].rearrange("p j q -> p q j"))
+
+        for h in range(HALVES):
+            stage(0, h)
+            round_pair(nc.vector.tensor_copy, 0, h)
+        nc.sync.dma_start(out_rows[:, 0:2, :], staged[0][:])
+        for h in range(HALVES):
+            multiply(LAST, h)
+        round_pair(nc.vector.tensor_copy, 1, 0)
+        round_pair(nc.scalar.copy, 1, 1)
+        for h in reversed(range(HALVES)):
+            stage(1, h)
+        nc.scalar.dma_start(out_rows[:, 2:4, :], staged[1][:])
         out_codes = sb.tile([P, Q], U32, name="out_codes", align_bytes=64)
         out_scales = sb.tile([P, Q], U8, name="out_scales", align_bytes=64)
-        for h, weight in enumerate((weight0, weight1)):
-            cols = slice(h * P, (h + 1) * P)
-            for j in range(PACK):
-                multiply(j, h, val_mx[j], weight)
-            nc.vector.tensor_copy(rounded[:, cols, :], result[h][:].rearrange("p j q -> p q j"))
-            staged = sb.tile([P, PACK, P], F32, name=f"staged{h}")
-            nc.scalar.copy(staged[:], result[h][:])
-            nc.scalar.dma_start(out_rows[:, :, cols], staged[:])
         for h in range(HALVES):
             cols = slice(h * P, (h + 1) * P)
             nc.vector.quantize_mx(
@@ -237,7 +236,8 @@ def tile_attend_sinkhorn_pl_kernel(tc, query, keys_words, keys_scales, fac, vals
             )
         nc.sync.dma_start(out_1[0].rearrange("p c t -> p (c t)").bitcast(I32), out_codes[:].bitcast(I32))
         for quad in range(4):
-            nc.sync.dma_start(
+            queue = nc.sync if quad % 2 == 0 else nc.scalar
+            queue.dma_start(
                 out_2[0, 4 * quad : 4 * quad + 4, :].bitcast(I32),
                 out_scales[32 * quad : 32 * quad + 4, :].bitcast(I32),
             )

@@ -115,16 +115,32 @@ def tile_attend_sinkhorn_pl_kernel(tc, query, keys_words, keys_scales, fac, vals
             )
             expd.append(tile)
             row_sum.append(col)
-        slots = []
-        for h in range(HALVES):
-            inv = sb.tile([P, 1], F32, name=f"row_inv{h}")
-            nc.vector.reciprocal(inv[:], row_sum[h][:])
-            tile = sb.tile([P, PACK, P], F32, name=f"rows{h}", align_bytes=64)
-            nc.vector.tensor_scalar(tile[:], expd[h][:], inv[:], None, ALU.mult)
-            bank = ps.tile([P, PACK, P], F32, name=f"slots{h}")
+        def turn_rows(bank, tile):
             for t in range(PACK):
                 nc.tensor.transpose(bank[:, t, :], tile[:, t, :], ident[:])
-            slots.append(bank)
+
+        row_inv = [sb.tile([P, 1], F32, name=f"row_inv{h}") for h in range(HALVES)]
+        rows = [sb.tile([P, PACK, P], F32, name=f"rows{h}", align_bytes=64) for h in range(HALVES)]
+        slots = [ps.tile([P, PACK, P], F32, name=f"slots{h}") for h in range(HALVES)]
+        nc.vector.reciprocal(row_inv[0][:], row_sum[0][:])
+        nc.vector.tensor_scalar(rows[0][:], expd[0][:], row_inv[0][:], None, ALU.mult)
+        turn_rows(slots[0], rows[0])
+        nc.vector.reciprocal(row_inv[1][:], row_sum[1][:])
+        both = sb.tile([P, PACK, P], F32, name="both", align_bytes=64)
+        for part in (slice(0, 2), slice(2, 4)):
+            nc.vector.scalar_tensor_tensor(
+                both[:, part, :], expd[1][:, part, :], row_inv[1][:], rows[0][:, part, :], ALU.mult, ALU.add
+            )
+        folded = ps.tile([P, PACK, P], F32, name="folded", tag="scores0")
+        turn_rows(folded, both)
+        nc.vector.tensor_scalar(rows[1][:], expd[1][:], row_inv[1][:], None, ALU.mult)
+        turn_rows(slots[1], rows[1])
+
+        def along_rows(col):
+            return col[:].unsqueeze(1).to_broadcast([P, P, PACK])
+
+        with_fac = sb.tile([P, P, PACK], F32, name="with_fac", align_bytes=64)
+        nc.vector.tensor_tensor(with_fac[:], slots[0][:].rearrange("p t q -> p q t"), along_rows(fac_rows), ALU.mult)
 
         def turn(picked, turned):
             pairs = picked.bitcast(F32)
@@ -143,25 +159,15 @@ def tile_attend_sinkhorn_pl_kernel(tc, query, keys_words, keys_scales, fac, vals
         picked2 = sb.tile([P, I], BF16, name="picked2", align_bytes=64)
         nc.scalar.activation(picked2[:], val_pool[2][:].indirect(offsets[:]), ACT.Copy)
 
-        part_sum = sb.tile([P, HALVES, PACK], F32, name="part_sum")
-        for h in range(HALVES):
-            nc.vector.tensor_reduce(part_sum[:, h, :], slots[h][:], AX.X, ALU.add)
         slot_sum = sb.tile([P, PACK], F32, name="slot_sum")
-        nc.vector.tensor_tensor(slot_sum[:], part_sum[:, 0, :], part_sum[:, 1, :], ALU.add)
+        nc.vector.tensor_reduce(slot_sum[:], folded[:], AX.X, ALU.add)
         slot_inv = sb.tile([P, PACK], F32, name="slot_inv")
         nc.vector.reciprocal(slot_inv[:], slot_sum[:])
         slot_gain = sb.tile([P, PACK], F32, name="slot_gain")
         nc.vector.tensor_tensor(slot_gain[:], slot_inv[:], fac_rows[:], ALU.mult)
-        weighed = []
-        for h in range(HALVES):
-            grouped = sb.tile([P, P, PACK], BF16, name=f"weight_grouped{h}", align_bytes=64)
-            nc.vector.tensor_tensor(
-                grouped[:],
-                slots[h][:].rearrange("p t q -> p q t"),
-                slot_gain[:].unsqueeze(1).to_broadcast([P, P, PACK]),
-                ALU.mult,
-            )
-            weighed.append(grouped)
+        weighed = [sb.tile([P, P, PACK], BF16, name=f"weighed{h}", align_bytes=64) for h in range(HALVES)]
+        nc.vector.tensor_tensor(weighed[0][:], with_fac[:], along_rows(slot_inv), ALU.mult)
+        nc.vector.tensor_tensor(weighed[1][:], slots[1][:].rearrange("p t q -> p q t"), along_rows(slot_gain), ALU.mult)
 
         turned01 = ps.tile([P, 4, P], F32, name="turned01", tag="scores1")
         for j in range(2):
@@ -171,7 +177,7 @@ def tile_attend_sinkhorn_pl_kernel(tc, query, keys_words, keys_scales, fac, vals
         turned2 = ps.tile([P, 2, P], F32, name="turned2", tag="scores0")
         turn(picked2[:], turned2[:])
 
-        picked3 = sb.tile([P, I], BF16, name="picked3", align_bytes=64)
+        picked3 = sb.tile([P, I], BF16, name="picked3", tag="picked3", align_bytes=64)
         nc.vector.tensor_copy(picked3[:, :SPLIT], val_pool[LAST][:].indirect(offsets[:, : SPLIT // 16]))
         nc.scalar.activation(picked3[:, SPLIT:], val_pool[LAST][:].indirect(offsets[:, SPLIT // 16 :]), ACT.Copy)
         turned3 = ps.tile([P, 2, P], F32, name="turned3", tag="scores1")
@@ -208,24 +214,26 @@ def tile_attend_sinkhorn_pl_kernel(tc, query, keys_words, keys_scales, fac, vals
         val_mx += quantize(grouped3[:], P, "val3")
         out_rows = out_0.rearrange("(p j) q -> p j q", j=PACK)
         rounded = sb.tile([P, Q, PACK], BF16, name="rounded", align_bytes=64)
-        staged = [sb.tile([P, 2, Q], F32, name=f"staged{pair}") for pair in range(2)]
+        staged = [
+            sb.tile([P, 2, Q], F32, name=f"staged{pair}", tag=tag, align_bytes=64)
+            for pair, tag in enumerate(("picked3", "staged1"))
+        ]
 
-        def stage(pair, h):
-            nc.scalar.copy(staged[pair][:, :, h * P : (h + 1) * P], result[pair][h][:])
+        def stage(copy, pair, h):
+            copy(staged[pair][:, :, h * P : (h + 1) * P], result[pair][h][:])
 
         def round_pair(copy, pair, h):
             copy(rounded[:, h * P : (h + 1) * P, 2 * pair : 2 * pair + 2], result[pair][h][:].rearrange("p j q -> p q j"))
 
         for h in range(HALVES):
-            stage(0, h)
-            round_pair(nc.vector.tensor_copy, 0, h)
+            stage(nc.scalar.copy, 0, h)
+            round_pair((nc.vector.tensor_copy, nc.scalar.copy)[h], 0, h)
         nc.sync.dma_start(out_rows[:, 0:2, :], staged[0][:])
         for h in range(HALVES):
             multiply(LAST, h)
-        round_pair(nc.vector.tensor_copy, 1, 0)
-        round_pair(nc.scalar.copy, 1, 1)
-        for h in reversed(range(HALVES)):
-            stage(1, h)
+        for h, copy in enumerate((nc.vector.tensor_copy, nc.scalar.copy)):
+            round_pair(copy, 1, h)
+            stage(copy, 1, h)
         nc.scalar.dma_start(out_rows[:, 2:4, :], staged[1][:])
         out_codes = sb.tile([P, Q], U32, name="out_codes", align_bytes=64)
         out_scales = sb.tile([P, Q], U8, name="out_scales", align_bytes=64)

@@ -22,26 +22,27 @@ P = 128
 PACK = 4
 HALVES = Q // P
 LAST = PACK - 1
-SPLIT = 160
+SPLIT = 192
 
 
 def tile_attend_sinkhorn_pl_kernel(tc, query, keys_words, keys_scales, fac, vals, offs, out_0, out_1, out_2):
     nc = tc.nc
     with ExitStack() as ctx:
         sb = ctx.enter_context(tc.tile_pool(name="sb", bufs=1))
+        after1 = ctx.enter_context(tc.tile_pool(name="after1", bufs=1))
         after2 = ctx.enter_context(tc.tile_pool(name="after2", bufs=1))
         after3 = ctx.enter_context(tc.tile_pool(name="after3", bufs=1))
         ps = ctx.enter_context(tc.psum_pool(name="ps", bufs=1))
 
-        offsets = sb.tile([P, I // 16], U16, name="offsets")
-        nc.sync.dma_start(offsets[:], offs)
         key_word_pool = sb.tile([P, T], U16, name="key_word_pool")
         nc.sync.dma_start(key_word_pool[:].bitcast(I32), keys_words[0].bitcast(I32))
-        fac_rows = sb.tile([P, PACK], F32, name="fac_rows")
-        nc.scalar.dma_start(fac_rows[:], fac.rearrange("(p t) o -> p (t o)", t=PACK))
+        offsets = sb.tile([P, I // 16], U16, name="offsets")
+        nc.sync.dma_start(offsets[:], offs)
 
         key_scale_pool = sb.tile([P, T], U8, name="key_scale_pool")
         nc.gpsimd.memset(key_scale_pool[:].bitcast(I32), 0)
+        fac_rows = sb.tile([P, PACK], F32, name="fac_rows")
+        nc.gpsimd.dma_start(fac_rows[:], fac.rearrange("(p t) o -> p (t o)", t=PACK))
         scale_rows = keys_scales[0].bitcast(I32).rearrange("(quad r) c -> r quad c", r=4)
         for r in range(4):
             nc.sync.dma_start(key_scale_pool[r:P:32, :].bitcast(I32), scale_rows[r])
@@ -49,7 +50,7 @@ def tile_attend_sinkhorn_pl_kernel(tc, query, keys_words, keys_scales, fac, vals
         nc.sync.dma_start(query_rows[:], query.rearrange("(p t) q -> p t q", t=PACK))
         val_planes = vals.rearrange("(p j) t -> j p t", j=PACK)
         val_pool = []
-        for j, pool in enumerate((sb, sb, after2, after3)):
+        for j, pool in enumerate((sb, after1, after2, after3)):
             if pool is sb:
                 plane = pool.tile([P, T], F32, name=f"val_pool{j}", align_bytes=64)
             else:
@@ -60,9 +61,9 @@ def tile_attend_sinkhorn_pl_kernel(tc, query, keys_words, keys_scales, fac, vals
         ident = sb.tile([P, P], F32, name="ident")
         make_identity(nc, ident[:])
 
-        def quantize(grouped, width, name, offset=None):
+        def quantize(grouped, width, name, offset=None, tag=""):
             if offset is None:
-                codes = sb.tile([P, width], U32, name=f"{name}_codes", align_bytes=64)
+                codes = sb.tile([P, width], U32, name=f"{name}_codes", tag=tag, align_bytes=64)
             else:
                 codes = after3.tile([P, width], U32, name=f"{name}_codes", offset=offset, align_bytes=64)
             scales = sb.tile([P, width], U8, name=f"{name}_scales", align_bytes=64)
@@ -115,26 +116,49 @@ def tile_attend_sinkhorn_pl_kernel(tc, query, keys_words, keys_scales, fac, vals
             )
             expd.append(tile)
             row_sum.append(col)
+        def turn(picked, turned):
+            pairs = picked.bitcast(F32)
+            for u in range(2):
+                nc.tensor.transpose(turned[:, u, :], pairs[:, u : I // 2 : 2], ident[:])
+
+        def group(grouped, turned, copy=nc.scalar.copy):
+            copy(
+                grouped.bitcast(F32).rearrange("p (j e u) -> p j e u", u=2, e=P),
+                turned.rearrange("p (j u) e -> p j e u", u=2),
+            )
+
+        picked0 = sb.tile([P, I], BF16, name="picked0", align_bytes=64)
+        nc.scalar.activation(picked0[:], val_pool[0][:].indirect(offsets[:]), ACT.Copy)
+        turned0 = ps.tile([P, 2, P], F32, name="turned0", tag="early0")
+        turn(picked0[:], turned0[:])
+
         def turn_rows(bank, tile):
             for t in range(PACK):
                 nc.tensor.transpose(bank[:, t, :], tile[:, t, :], ident[:])
 
         row_inv = [sb.tile([P, 1], F32, name=f"row_inv{h}") for h in range(HALVES)]
-        rows = [sb.tile([P, PACK, P], F32, name=f"rows{h}", align_bytes=64) for h in range(HALVES)]
-        slots = [ps.tile([P, PACK, P], F32, name=f"slots{h}") for h in range(HALVES)]
+        rows = [
+            sb.tile([P, PACK, P], F32, name="rows0", align_bytes=64),
+            after1.tile([P, PACK, P], F32, name="rows1", offset=0, align_bytes=64),
+        ]
+        slots = [ps.tile([P, PACK, P], F32, name=f"slots{h}", tag=f"slots{h}") for h in range(HALVES)]
         nc.vector.reciprocal(row_inv[0][:], row_sum[0][:])
         nc.vector.tensor_scalar(rows[0][:], expd[0][:], row_inv[0][:], None, ALU.mult)
         turn_rows(slots[0], rows[0])
         nc.vector.reciprocal(row_inv[1][:], row_sum[1][:])
-        both = sb.tile([P, PACK, P], F32, name="both", align_bytes=64)
-        for part in (slice(0, 2), slice(2, 4)):
+        grouped0 = sb.tile([P, I], BF16, name="grouped0", tag="neg_max1", align_bytes=64)
+        group(grouped0[:], turned0[:], nc.vector.tensor_copy)
+        both = sb.tile([P, PACK, P], F32, name="both", tag="both", align_bytes=64)
+        folded = []
+        for a, tag in enumerate(("scores0", "late0")):
+            part = slice(2 * a, 2 * a + 2)
             nc.vector.scalar_tensor_tensor(
                 both[:, part, :], expd[1][:, part, :], row_inv[1][:], rows[0][:, part, :], ALU.mult, ALU.add
             )
-        folded = ps.tile([P, PACK, P], F32, name="folded", tag="scores0")
-        turn_rows(folded, both)
-        nc.vector.tensor_scalar(rows[1][:], expd[1][:], row_inv[1][:], None, ALU.mult)
-        turn_rows(slots[1], rows[1])
+            bank = ps.tile([P, 2, P], F32, name=f"folded{a}", tag=tag)
+            for t in range(2):
+                nc.tensor.transpose(bank[:, t, :], both[:, 2 * a + t, :], ident[:])
+            folded.append(bank)
 
         def along_rows(col):
             return col[:].unsqueeze(1).to_broadcast([P, P, PACK])
@@ -142,25 +166,17 @@ def tile_attend_sinkhorn_pl_kernel(tc, query, keys_words, keys_scales, fac, vals
         with_fac = sb.tile([P, P, PACK], F32, name="with_fac", align_bytes=64)
         nc.vector.tensor_tensor(with_fac[:], slots[0][:].rearrange("p t q -> p q t"), along_rows(fac_rows), ALU.mult)
 
-        def turn(picked, turned):
-            pairs = picked.bitcast(F32)
-            for u in range(2):
-                nc.tensor.transpose(turned[:, u, :], pairs[:, u : I // 2 : 2], ident[:])
-
-        def group(grouped, turned):
-            nc.scalar.copy(
-                grouped.bitcast(F32).rearrange("p (j e u) -> p j e u", u=2, e=P),
-                turned.rearrange("p (j u) e -> p j e u", u=2),
-            )
-
-        picked01 = sb.tile([P, 2, I], BF16, name="picked01", align_bytes=64)
-        for j in range(2):
-            nc.scalar.activation(picked01[:, j, :], val_pool[j][:].indirect(offsets[:]), ACT.Copy)
+        picked1 = sb.tile([P, I], BF16, name="picked1", align_bytes=64)
+        nc.scalar.activation(picked1[:], val_pool[1][:].indirect(offsets[:]), ACT.Copy)
+        nc.scalar.activation(rows[1][:], expd[1][:], ACT.Copy, scale=row_inv[1][:])
+        turn_rows(slots[1], rows[1])
         picked2 = sb.tile([P, I], BF16, name="picked2", align_bytes=64)
         nc.scalar.activation(picked2[:], val_pool[2][:].indirect(offsets[:]), ACT.Copy)
 
         slot_sum = sb.tile([P, PACK], F32, name="slot_sum")
-        nc.vector.tensor_reduce(slot_sum[:], folded[:], AX.X, ALU.add)
+        for a in range(2):
+            nc.vector.tensor_reduce(slot_sum[:, 2 * a : 2 * a + 2], folded[a][:], AX.X, ALU.add)
+        val_mx = quantize(grouped0[:], P, "val0", tag="both")
         slot_inv = sb.tile([P, PACK], F32, name="slot_inv")
         nc.vector.reciprocal(slot_inv[:], slot_sum[:])
         slot_gain = sb.tile([P, PACK], F32, name="slot_gain")
@@ -169,72 +185,67 @@ def tile_attend_sinkhorn_pl_kernel(tc, query, keys_words, keys_scales, fac, vals
         nc.vector.tensor_tensor(weighed[0][:], with_fac[:], along_rows(slot_inv), ALU.mult)
         nc.vector.tensor_tensor(weighed[1][:], slots[1][:].rearrange("p t q -> p q t"), along_rows(slot_gain), ALU.mult)
 
-        turned01 = ps.tile([P, 4, P], F32, name="turned01", tag="scores1")
-        for j in range(2):
-            turn(picked01[:, j, :], turned01[:, 2 * j : 2 * j + 2, :])
-        grouped01 = after2.tile([P, 2 * I], BF16, name="grouped01", offset=0, align_bytes=64)
-        group(grouped01[:], turned01[:])
-        turned2 = ps.tile([P, 2, P], F32, name="turned2", tag="scores0")
+        turned1 = ps.tile([P, 2, P], F32, name="turned1", tag="scores0")
+        turn(picked1[:], turned1[:])
+        grouped1 = after2.tile([P, I], BF16, name="grouped1", offset=0, align_bytes=64)
+        group(grouped1[:], turned1[:])
+        turned2 = ps.tile([P, 2, P], F32, name="turned2", tag="scores1")
         turn(picked2[:], turned2[:])
 
-        picked3 = sb.tile([P, I], BF16, name="picked3", tag="picked3", align_bytes=64)
+        picked3 = sb.tile([P, I], BF16, name="picked3", align_bytes=64)
         nc.vector.tensor_copy(picked3[:, :SPLIT], val_pool[LAST][:].indirect(offsets[:, : SPLIT // 16]))
         nc.scalar.activation(picked3[:, SPLIT:], val_pool[LAST][:].indirect(offsets[:, SPLIT // 16 :]), ACT.Copy)
-        turned3 = ps.tile([P, 2, P], F32, name="turned3", tag="scores1")
+        turned3 = ps.tile([P, 2, P], F32, name="turned3", tag="scores0")
         turn(picked3[:], turned3[:])
         grouped2 = after3.tile([P, I], BF16, name="grouped2", offset=0, align_bytes=64)
         group(grouped2[:], turned2[:])
-        weight_mx = quantize(weighed[0][:].rearrange("p q t -> p (q t)"), P, "weight0", 1024)
-        val_mx = quantize(grouped01[:], 2 * P, "val01", 2048)
+        weight_mx = quantize(weighed[0][:].rearrange("p q t -> p (q t)"), P, "weight0")
+        val_mx += quantize(grouped1[:], P, "val1")
         weight_mx += quantize(weighed[1][:].rearrange("p q t -> p (q t)"), P, "weight1", 1536)
         val_mx += quantize(grouped2[:], P, "val2")
 
+        groups = (slice(0, 2), slice(2, 3), slice(3, 4))
         result = [
-            [ps.tile([P, 2, P], F32, name=f"result{pair}{h}") for h in range(HALVES)] for pair in range(2)
+            [ps.tile([P, js.stop - js.start, P], F32, name=f"{tag}{h}", tag=f"{tag}{h}") for h in range(HALVES)]
+            for js, tag in zip(groups, ("early", "slots", "late"))
         ]
 
-        def multiply(j, h):
-            nc.tensor.matmul_mx(
-                out=result[j // 2][h][:, j % 2, :],
-                lhsT=val_mx[j][0].bitcast(FP8X4),
-                lhsT_scale=val_mx[j][1],
-                rhs=weight_mx[h][0].bitcast(FP8X4),
-                rhs_scale=weight_mx[h][1],
-                start=True,
-                stop=True,
-            )
+        def multiply(g):
+            for h in range(HALVES):
+                for j in range(groups[g].start, groups[g].stop):
+                    nc.tensor.matmul_mx(
+                        out=result[g][h][:, j - groups[g].start, :],
+                        lhsT=val_mx[j][0].bitcast(FP8X4),
+                        lhsT_scale=val_mx[j][1],
+                        rhs=weight_mx[h][0].bitcast(FP8X4),
+                        rhs_scale=weight_mx[h][1],
+                        start=True,
+                        stop=True,
+                    )
 
-        for h in range(HALVES):
-            for j in range(2):
-                multiply(j, h)
-        for h in range(HALVES):
-            multiply(2, h)
+        out_rows = out_0.rearrange("(p j) q -> p j q", j=PACK)
+        rounded = after3.tile([P, Q, PACK], BF16, name="rounded", offset=2048, align_bytes=64)
+
+        def hand_out(g, queue):
+            js = groups[g]
+            staged = after3.tile(
+                [P, js.stop - js.start, Q], F32, name=f"staged{g}", offset=4096 + 1024 * js.start, align_bytes=64
+            )
+            for h, copy in enumerate((nc.vector.tensor_copy, nc.scalar.copy)):
+                cols = slice(h * P, (h + 1) * P)
+                copy(rounded[:, cols, js], result[g][h][:].rearrange("p j q -> p q j"))
+                copy(staged[:, :, cols], result[g][h][:])
+            queue.dma_start(out_rows[:, js, :], staged[:])
+
+        multiply(0)
+        multiply(1)
         grouped3 = sb.tile([P, I], BF16, name="grouped3", align_bytes=64)
         group(grouped3[:], turned3[:])
         val_mx += quantize(grouped3[:], P, "val3")
-        out_rows = out_0.rearrange("(p j) q -> p j q", j=PACK)
-        rounded = sb.tile([P, Q, PACK], BF16, name="rounded", align_bytes=64)
-        staged = [
-            sb.tile([P, 2, Q], F32, name=f"staged{pair}", tag=tag, align_bytes=64)
-            for pair, tag in enumerate(("picked3", "staged1"))
-        ]
-
-        def stage(copy, pair, h):
-            copy(staged[pair][:, :, h * P : (h + 1) * P], result[pair][h][:])
-
-        def round_pair(copy, pair, h):
-            copy(rounded[:, h * P : (h + 1) * P, 2 * pair : 2 * pair + 2], result[pair][h][:].rearrange("p j q -> p q j"))
-
-        for h in range(HALVES):
-            stage(nc.scalar.copy, 0, h)
-            round_pair((nc.vector.tensor_copy, nc.scalar.copy)[h], 0, h)
-        nc.sync.dma_start(out_rows[:, 0:2, :], staged[0][:])
-        for h in range(HALVES):
-            multiply(LAST, h)
-        for h, copy in enumerate((nc.vector.tensor_copy, nc.scalar.copy)):
-            round_pair(copy, 1, h)
-            stage(copy, 1, h)
-        nc.scalar.dma_start(out_rows[:, 2:4, :], staged[1][:])
+        multiply(2)
+        hand_out(0, nc.sync)
+        hand_out(1, nc.sync)
+        hand_out(2, nc.sync)
         out_codes = sb.tile([P, Q], U32, name="out_codes", align_bytes=64)
         out_scales = sb.tile([P, Q], U8, name="out_scales", align_bytes=64)
         for h in range(HALVES):

@@ -22,7 +22,7 @@ P = 128
 PACK = 4
 HALVES = Q // P
 LAST = PACK - 1
-SPLIT = 192
+SPLIT = 224
 
 
 def tile_attend_sinkhorn_pl_kernel(tc, query, keys_words, keys_scales, fac, vals, offs, out_0, out_1, out_2):
@@ -30,7 +30,7 @@ def tile_attend_sinkhorn_pl_kernel(tc, query, keys_words, keys_scales, fac, vals
     with ExitStack() as ctx:
         sb = ctx.enter_context(tc.tile_pool(name="sb", bufs=1))
         after1 = ctx.enter_context(tc.tile_pool(name="after1", bufs=1))
-        after2 = ctx.enter_context(tc.tile_pool(name="after2", bufs=1))
+        after_sums = ctx.enter_context(tc.tile_pool(name="after_sums", bufs=1))
         after3 = ctx.enter_context(tc.tile_pool(name="after3", bufs=1))
         ps = ctx.enter_context(tc.psum_pool(name="ps", bufs=1))
 
@@ -50,7 +50,7 @@ def tile_attend_sinkhorn_pl_kernel(tc, query, keys_words, keys_scales, fac, vals
         nc.sync.dma_start(query_rows[:], query.rearrange("(p t) q -> p t q", t=PACK))
         val_planes = vals.rearrange("(p j) t -> j p t", j=PACK)
         val_pool = []
-        for j, pool in enumerate((sb, after1, after2, after3)):
+        for j, pool in enumerate((sb, after1, sb, after3)):
             if pool is sb:
                 plane = pool.tile([P, T], F32, name=f"val_pool{j}", align_bytes=64)
             else:
@@ -61,11 +61,11 @@ def tile_attend_sinkhorn_pl_kernel(tc, query, keys_words, keys_scales, fac, vals
         ident = sb.tile([P, P], F32, name="ident")
         make_identity(nc, ident[:])
 
-        def quantize(grouped, width, name, offset=None, tag=""):
+        def quantize(grouped, width, name, offset=None, pool=after3):
             if offset is None:
-                codes = sb.tile([P, width], U32, name=f"{name}_codes", tag=tag, align_bytes=64)
+                codes = sb.tile([P, width], U32, name=f"{name}_codes", align_bytes=64)
             else:
-                codes = after3.tile([P, width], U32, name=f"{name}_codes", offset=offset, align_bytes=64)
+                codes = pool.tile([P, width], U32, name=f"{name}_codes", offset=offset, align_bytes=64)
             scales = sb.tile([P, width], U8, name=f"{name}_scales", align_bytes=64)
             nc.vector.quantize_mx(codes[:].bitcast(FP8X4), scales[:], grouped)
             return [(codes[:, a : a + P], scales[:, a : a + P]) for a in range(0, width, P)]
@@ -148,54 +148,67 @@ def tile_attend_sinkhorn_pl_kernel(tc, query, keys_words, keys_scales, fac, vals
         nc.vector.reciprocal(row_inv[1][:], row_sum[1][:])
         grouped0 = sb.tile([P, I], BF16, name="grouped0", tag="neg_max1", align_bytes=64)
         group(grouped0[:], turned0[:], nc.vector.tensor_copy)
-        both = sb.tile([P, PACK, P], F32, name="both", tag="both", align_bytes=64)
+        both = after_sums.tile([P, PACK, P], F32, name="both", offset=0, align_bytes=64)
         folded = []
         for a, tag in enumerate(("scores0", "late0")):
-            part = slice(2 * a, 2 * a + 2)
-            nc.vector.scalar_tensor_tensor(
-                both[:, part, :], expd[1][:, part, :], row_inv[1][:], rows[0][:, part, :], ALU.mult, ALU.add
-            )
             bank = ps.tile([P, 2, P], F32, name=f"folded{a}", tag=tag)
-            for t in range(2):
-                nc.tensor.transpose(bank[:, t, :], both[:, 2 * a + t, :], ident[:])
+            for t in range(2 * a, 2 * a + 2):
+                nc.vector.scalar_tensor_tensor(
+                    both[:, t, :], expd[1][:, t, :], row_inv[1][:], rows[0][:, t, :], ALU.mult, ALU.add
+                )
+                nc.tensor.transpose(bank[:, t - 2 * a, :], both[:, t, :], ident[:])
             folded.append(bank)
 
-        def along_rows(col):
-            return col[:].unsqueeze(1).to_broadcast([P, P, PACK])
+        def along_rows(col, count):
+            return col[:].unsqueeze(1).to_broadcast([P, count, PACK])
 
-        with_fac = sb.tile([P, P, PACK], F32, name="with_fac", align_bytes=64)
-        nc.vector.tensor_tensor(with_fac[:], slots[0][:].rearrange("p t q -> p q t"), along_rows(fac_rows), ALU.mult)
+        def times_fac(part, pool, **place):
+            tile = pool.tile([P, P // 2, PACK], F32, name=f"with_fac{part}", align_bytes=64, **place)
+            cols = slice(part * P // 2, (part + 1) * P // 2)
+            nc.vector.tensor_tensor(
+                tile[:], slots[0][:, :, cols].rearrange("p t q -> p q t"), along_rows(fac_rows, P // 2), ALU.mult
+            )
+            return tile
+
+        with_fac = [times_fac(0, sb)]
 
         picked1 = sb.tile([P, I], BF16, name="picked1", align_bytes=64)
         nc.scalar.activation(picked1[:], val_pool[1][:].indirect(offsets[:]), ACT.Copy)
+        turned1 = ps.tile([P, 2, P], F32, name="turned1", tag="scores1")
+        turn(picked1[:], turned1[:])
         nc.scalar.activation(rows[1][:], expd[1][:], ACT.Copy, scale=row_inv[1][:])
         turn_rows(slots[1], rows[1])
+        grouped1 = sb.tile([P, I], BF16, name="grouped1", align_bytes=64)
+        group(grouped1[:], turned1[:])
         picked2 = sb.tile([P, I], BF16, name="picked2", align_bytes=64)
         nc.scalar.activation(picked2[:], val_pool[2][:].indirect(offsets[:]), ACT.Copy)
 
         slot_sum = sb.tile([P, PACK], F32, name="slot_sum")
         for a in range(2):
             nc.vector.tensor_reduce(slot_sum[:, 2 * a : 2 * a + 2], folded[a][:], AX.X, ALU.add)
-        val_mx = quantize(grouped0[:], P, "val0", tag="both")
+        with_fac.append(times_fac(1, after_sums, offset=0))
         slot_inv = sb.tile([P, PACK], F32, name="slot_inv")
         nc.vector.reciprocal(slot_inv[:], slot_sum[:])
+        val_mx = quantize(grouped0[:], P, "val0", 1024, after_sums)
         slot_gain = sb.tile([P, PACK], F32, name="slot_gain")
         nc.vector.tensor_tensor(slot_gain[:], slot_inv[:], fac_rows[:], ALU.mult)
         weighed = [sb.tile([P, P, PACK], BF16, name=f"weighed{h}", align_bytes=64) for h in range(HALVES)]
-        nc.vector.tensor_tensor(weighed[0][:], with_fac[:], along_rows(slot_inv), ALU.mult)
-        nc.vector.tensor_tensor(weighed[1][:], slots[1][:].rearrange("p t q -> p q t"), along_rows(slot_gain), ALU.mult)
+        for part in range(2):
+            nc.vector.tensor_tensor(
+                weighed[0][:, part * P // 2 : (part + 1) * P // 2, :],
+                with_fac[part][:],
+                along_rows(slot_inv, P // 2),
+                ALU.mult,
+            )
+        nc.vector.tensor_tensor(weighed[1][:], slots[1][:].rearrange("p t q -> p q t"), along_rows(slot_gain, P), ALU.mult)
 
-        turned1 = ps.tile([P, 2, P], F32, name="turned1", tag="scores0")
-        turn(picked1[:], turned1[:])
-        grouped1 = after2.tile([P, I], BF16, name="grouped1", offset=0, align_bytes=64)
-        group(grouped1[:], turned1[:])
-        turned2 = ps.tile([P, 2, P], F32, name="turned2", tag="scores1")
+        turned2 = ps.tile([P, 2, P], F32, name="turned2", tag="scores0")
         turn(picked2[:], turned2[:])
 
         picked3 = sb.tile([P, I], BF16, name="picked3", align_bytes=64)
         nc.vector.tensor_copy(picked3[:, :SPLIT], val_pool[LAST][:].indirect(offsets[:, : SPLIT // 16]))
         nc.scalar.activation(picked3[:, SPLIT:], val_pool[LAST][:].indirect(offsets[:, SPLIT // 16 :]), ACT.Copy)
-        turned3 = ps.tile([P, 2, P], F32, name="turned3", tag="scores0")
+        turned3 = ps.tile([P, 2, P], F32, name="turned3", tag="scores1")
         turn(picked3[:], turned3[:])
         grouped2 = after3.tile([P, I], BF16, name="grouped2", offset=0, align_bytes=64)
         group(grouped2[:], turned2[:])

@@ -23,14 +23,15 @@ PACK = 4
 HALVES = Q // P
 LAST = PACK - 1
 SPLIT = 224
+AHEAD = 64
 
 
 def tile_attend_sinkhorn_pl_kernel(tc, query, keys_words, keys_scales, fac, vals, offs, out_0, out_1, out_2):
     nc = tc.nc
     with ExitStack() as ctx:
         sb = ctx.enter_context(tc.tile_pool(name="sb", bufs=1))
-        after1 = ctx.enter_context(tc.tile_pool(name="after1", bufs=1))
         after_sums = ctx.enter_context(tc.tile_pool(name="after_sums", bufs=1))
+        after2 = ctx.enter_context(tc.tile_pool(name="after2", bufs=1))
         after3 = ctx.enter_context(tc.tile_pool(name="after3", bufs=1))
         ps = ctx.enter_context(tc.psum_pool(name="ps", bufs=1))
 
@@ -50,7 +51,7 @@ def tile_attend_sinkhorn_pl_kernel(tc, query, keys_words, keys_scales, fac, vals
         nc.sync.dma_start(query_rows[:], query.rearrange("(p t) q -> p t q", t=PACK))
         val_planes = vals.rearrange("(p j) t -> j p t", j=PACK)
         val_pool = []
-        for j, pool in enumerate((sb, after1, sb, after3)):
+        for j, pool in enumerate((sb, sb, after2, after3)):
             if pool is sb:
                 plane = pool.tile([P, T], F32, name=f"val_pool{j}", align_bytes=64)
             else:
@@ -137,10 +138,7 @@ def tile_attend_sinkhorn_pl_kernel(tc, query, keys_words, keys_scales, fac, vals
                 nc.tensor.transpose(bank[:, t, :], tile[:, t, :], ident[:])
 
         row_inv = [sb.tile([P, 1], F32, name=f"row_inv{h}") for h in range(HALVES)]
-        rows = [
-            sb.tile([P, PACK, P], F32, name="rows0", align_bytes=64),
-            after1.tile([P, PACK, P], F32, name="rows1", offset=0, align_bytes=64),
-        ]
+        rows = [sb.tile([P, PACK, P], F32, name=f"rows{h}", tag="rows", align_bytes=64) for h in range(HALVES)]
         slots = [ps.tile([P, PACK, P], F32, name=f"slots{h}", tag=f"slots{h}") for h in range(HALVES)]
         nc.vector.reciprocal(row_inv[0][:], row_sum[0][:])
         nc.vector.tensor_scalar(rows[0][:], expd[0][:], row_inv[0][:], None, ALU.mult)
@@ -152,63 +150,59 @@ def tile_attend_sinkhorn_pl_kernel(tc, query, keys_words, keys_scales, fac, vals
         folded = []
         for a, tag in enumerate(("scores0", "late0")):
             bank = ps.tile([P, 2, P], F32, name=f"folded{a}", tag=tag)
-            for t in range(2 * a, 2 * a + 2):
+            for part in (slice(2 * a, 2 * a + 2),):
                 nc.vector.scalar_tensor_tensor(
-                    both[:, t, :], expd[1][:, t, :], row_inv[1][:], rows[0][:, t, :], ALU.mult, ALU.add
+                    both[:, part, :], expd[1][:, part, :], row_inv[1][:], rows[0][:, part, :], ALU.mult, ALU.add
                 )
-                nc.tensor.transpose(bank[:, t - 2 * a, :], both[:, t, :], ident[:])
+                for t in range(part.start, part.stop):
+                    nc.tensor.transpose(bank[:, t - 2 * a, :], both[:, t, :], ident[:])
             folded.append(bank)
+
+        nc.gpsimd.tensor_scalar(rows[1][:], expd[1][:], row_inv[1][:], 1.0, ALU.mult, ALU.mult)
+        turn_rows(slots[1], rows[1])
 
         def along_rows(col, count):
             return col[:].unsqueeze(1).to_broadcast([P, count, PACK])
 
-        def times_fac(part, pool, **place):
-            tile = pool.tile([P, P // 2, PACK], F32, name=f"with_fac{part}", align_bytes=64, **place)
-            cols = slice(part * P // 2, (part + 1) * P // 2)
-            nc.vector.tensor_tensor(
-                tile[:], slots[0][:, :, cols].rearrange("p t q -> p q t"), along_rows(fac_rows, P // 2), ALU.mult
-            )
-            return tile
-
-        with_fac = [times_fac(0, sb)]
+        with_fac = sb.tile([P, AHEAD, PACK], F32, name="with_fac", align_bytes=64)
+        nc.vector.tensor_tensor(
+            with_fac[:], slots[0][:, :, :AHEAD].rearrange("p t q -> p q t"), along_rows(fac_rows, AHEAD), ALU.mult
+        )
 
         picked1 = sb.tile([P, I], BF16, name="picked1", align_bytes=64)
         nc.scalar.activation(picked1[:], val_pool[1][:].indirect(offsets[:]), ACT.Copy)
-        turned1 = ps.tile([P, 2, P], F32, name="turned1", tag="scores1")
-        turn(picked1[:], turned1[:])
-        nc.scalar.activation(rows[1][:], expd[1][:], ACT.Copy, scale=row_inv[1][:])
-        turn_rows(slots[1], rows[1])
-        grouped1 = sb.tile([P, I], BF16, name="grouped1", align_bytes=64)
-        group(grouped1[:], turned1[:])
         picked2 = sb.tile([P, I], BF16, name="picked2", align_bytes=64)
         nc.scalar.activation(picked2[:], val_pool[2][:].indirect(offsets[:]), ACT.Copy)
 
         slot_sum = sb.tile([P, PACK], F32, name="slot_sum")
         for a in range(2):
             nc.vector.tensor_reduce(slot_sum[:, 2 * a : 2 * a + 2], folded[a][:], AX.X, ALU.add)
-        with_fac.append(times_fac(1, after_sums, offset=0))
         slot_inv = sb.tile([P, PACK], F32, name="slot_inv")
+        val_mx = quantize(grouped0[:], P, "val0", 0, after_sums)
         nc.vector.reciprocal(slot_inv[:], slot_sum[:])
-        val_mx = quantize(grouped0[:], P, "val0", 1024, after_sums)
         slot_gain = sb.tile([P, PACK], F32, name="slot_gain")
         nc.vector.tensor_tensor(slot_gain[:], slot_inv[:], fac_rows[:], ALU.mult)
         weighed = [sb.tile([P, P, PACK], BF16, name=f"weighed{h}", align_bytes=64) for h in range(HALVES)]
-        for part in range(2):
-            nc.vector.tensor_tensor(
-                weighed[0][:, part * P // 2 : (part + 1) * P // 2, :],
-                with_fac[part][:],
-                along_rows(slot_inv, P // 2),
-                ALU.mult,
-            )
+        nc.vector.tensor_tensor(weighed[0][:, :AHEAD, :], with_fac[:], along_rows(slot_inv, AHEAD), ALU.mult)
+        nc.vector.tensor_tensor(
+            weighed[0][:, AHEAD:, :],
+            slots[0][:, :, AHEAD:].rearrange("p t q -> p q t"),
+            along_rows(slot_gain, P - AHEAD),
+            ALU.mult,
+        )
         nc.vector.tensor_tensor(weighed[1][:], slots[1][:].rearrange("p t q -> p q t"), along_rows(slot_gain, P), ALU.mult)
 
-        turned2 = ps.tile([P, 2, P], F32, name="turned2", tag="scores0")
+        turned1 = ps.tile([P, 2, P], F32, name="turned1", tag="scores0")
+        turn(picked1[:], turned1[:])
+        grouped1 = after2.tile([P, I], BF16, name="grouped1", offset=0, align_bytes=64)
+        group(grouped1[:], turned1[:])
+        turned2 = ps.tile([P, 2, P], F32, name="turned2", tag="scores1")
         turn(picked2[:], turned2[:])
 
         picked3 = sb.tile([P, I], BF16, name="picked3", align_bytes=64)
         nc.vector.tensor_copy(picked3[:, :SPLIT], val_pool[LAST][:].indirect(offsets[:, : SPLIT // 16]))
         nc.scalar.activation(picked3[:, SPLIT:], val_pool[LAST][:].indirect(offsets[:, SPLIT // 16 :]), ACT.Copy)
-        turned3 = ps.tile([P, 2, P], F32, name="turned3", tag="scores1")
+        turned3 = ps.tile([P, 2, P], F32, name="turned3", tag="scores0")
         turn(picked3[:], turned3[:])
         grouped2 = after3.tile([P, I], BF16, name="grouped2", offset=0, align_bytes=64)
         group(grouped2[:], turned2[:])

@@ -22,8 +22,12 @@ P = 128
 PACK = 4
 HALVES = Q // P
 LAST = PACK - 1
-SPLIT = 224
+LIST_ROWS = 16
+QUADS, QUAD = 4, 32
+KIB = 1024
+VECTOR_SHARE = 96
 AHEAD = 64
+GROUPS = (slice(0, 2), slice(2, 3), slice(3, 4))
 
 
 def tile_attend_sinkhorn_pl_kernel(tc, query, keys_words, keys_scales, fac, vals, offs, out_0, out_1, out_2):
@@ -37,7 +41,7 @@ def tile_attend_sinkhorn_pl_kernel(tc, query, keys_words, keys_scales, fac, vals
 
         key_word_pool = sb.tile([P, T], U16, name="key_word_pool")
         nc.sync.dma_start(key_word_pool[:].bitcast(I32), keys_words[0].bitcast(I32))
-        offsets = sb.tile([P, I // 16], U16, name="offsets")
+        offsets = sb.tile([P, I // LIST_ROWS], U16, name="offsets")
         nc.sync.dma_start(offsets[:], offs)
 
         key_scale_pool = sb.tile([P, T], U8, name="key_scale_pool")
@@ -46,30 +50,27 @@ def tile_attend_sinkhorn_pl_kernel(tc, query, keys_words, keys_scales, fac, vals
         nc.gpsimd.dma_start(fac_rows[:], fac.rearrange("(p t) o -> p (t o)", t=PACK))
         scale_rows = keys_scales[0].bitcast(I32).rearrange("(quad r) c -> r quad c", r=4)
         for r in range(4):
-            nc.sync.dma_start(key_scale_pool[r:P:32, :].bitcast(I32), scale_rows[r])
+            nc.sync.dma_start(key_scale_pool[r:P:QUAD, :].bitcast(I32), scale_rows[r])
         query_rows = sb.tile([P, PACK, Q], F32, name="query_rows")
         nc.sync.dma_start(query_rows[:], query.rearrange("(p t) q -> p t q", t=PACK))
         val_planes = vals.rearrange("(p j) t -> j p t", j=PACK)
         val_pool = []
-        for j, pool in enumerate((sb, sb, after2, after3)):
-            if pool is sb:
-                plane = pool.tile([P, T], F32, name=f"val_pool{j}", align_bytes=64)
-            else:
-                plane = pool.tile([P, T], F32, name=f"val_pool{j}", offset=0, align_bytes=64)
+        for j, (pool, place) in enumerate(((sb, None), (sb, None), (after2, 0), (after3, 0))):
+            plane = pool.tile([P, T], F32, name=f"val_pool{j}", offset=place, align_bytes=64)
             nc.sync.dma_start(plane[:], val_planes[j])
             val_pool.append(plane)
 
         ident = sb.tile([P, P], F32, name="ident")
         make_identity(nc, ident[:])
 
-        def quantize(grouped, width, name, offset=None, pool=after3):
-            if offset is None:
-                codes = sb.tile([P, width], U32, name=f"{name}_codes", align_bytes=64)
-            else:
-                codes = pool.tile([P, width], U32, name=f"{name}_codes", offset=offset, align_bytes=64)
-            scales = sb.tile([P, width], U8, name=f"{name}_scales", align_bytes=64)
+        def quantize(grouped, name, pool=sb, place=None):
+            codes = pool.tile([P, P], U32, name=f"{name}_codes", offset=place, align_bytes=64)
+            scales = sb.tile([P, P], U8, name=f"{name}_scales", align_bytes=64)
             nc.vector.quantize_mx(codes[:].bitcast(FP8X4), scales[:], grouped)
-            return [(codes[:, a : a + P], scales[:, a : a + P]) for a in range(0, width, P)]
+            return codes, scales
+
+        def flat(tile):
+            return tile.rearrange("p q t -> p (q t)")
 
         key_words = sb.tile([P, I], U16, name="key_words", align_bytes=64)
         nc.vector.tensor_copy(key_words[:], key_word_pool[:].indirect(offsets[:]))
@@ -78,21 +79,21 @@ def tile_attend_sinkhorn_pl_kernel(tc, query, keys_words, keys_scales, fac, vals
         query_grouped = []
         for h in range(HALVES):
             grouped = sb.tile([P, P, PACK], BF16, name=f"query_grouped{h}", align_bytes=64)
-            dst = grouped[:].rearrange("p (c i) t -> p c t i", i=4)
-            src = query_rows[:, :, h * P : (h + 1) * P].rearrange("p t (c i) -> p c t i", i=4)
-            nc.scalar.activation(dst, src, ACT.Copy)
+            nc.scalar.activation(
+                grouped[:].rearrange("p (c i) t -> p c t i", i=4),
+                query_rows[:, :, h * P : (h + 1) * P].rearrange("p t (c i) -> p c t i", i=4),
+                ACT.Copy,
+            )
             query_grouped.append(grouped)
-        query_mx = [
-            quantize(query_grouped[h][:].rearrange("p q t -> p (q t)"), P, f"query{h}")[0] for h in range(HALVES)
-        ]
+        query_mx = [quantize(flat(query_grouped[h][:]), f"query{h}") for h in range(HALVES)]
 
         scores, neg_max = [], []
         for h in range(HALVES):
             bank = ps.tile([P, I], F32, name=f"scores{h}", tag=f"scores{h}")
             nc.tensor.matmul_mx(
                 out=bank[:],
-                lhsT=query_mx[h][0].bitcast(FP8X4),
-                lhsT_scale=query_mx[h][1],
+                lhsT=query_mx[h][0][:].bitcast(FP8X4),
+                lhsT_scale=query_mx[h][1][:],
                 rhs=key_words[:].bitcast(FP4X4),
                 rhs_scale=key_scales[:],
                 start=True,
@@ -117,25 +118,36 @@ def tile_attend_sinkhorn_pl_kernel(tc, query, keys_words, keys_scales, fac, vals
             )
             expd.append(tile)
             row_sum.append(col)
-        def turn(picked, turned):
-            pairs = picked.bitcast(F32)
+
+        def gather_on_scalar(j):
+            picked = sb.tile([P, I], BF16, name=f"picked{j}", align_bytes=64)
+            nc.scalar.activation(picked[:], val_pool[j][:].indirect(offsets[:]), ACT.Copy)
+            return picked
+
+        def turn(picked, j, tag):
+            turned = ps.tile([P, 2, P], F32, name=f"turned{j}", tag=tag)
+            pairs = picked[:].bitcast(F32)
             for u in range(2):
                 nc.tensor.transpose(turned[:, u, :], pairs[:, u : I // 2 : 2], ident[:])
+            return turned
 
-        def group(grouped, turned, copy=nc.scalar.copy):
+        def group(grouped, turned, copy):
             copy(
-                grouped.bitcast(F32).rearrange("p (j e u) -> p j e u", u=2, e=P),
-                turned.rearrange("p (j u) e -> p j e u", u=2),
+                grouped[:].bitcast(F32).rearrange("p (e u) -> p e u", u=2),
+                turned[:].rearrange("p u e -> p e u"),
             )
-
-        picked0 = sb.tile([P, I], BF16, name="picked0", align_bytes=64)
-        nc.scalar.activation(picked0[:], val_pool[0][:].indirect(offsets[:]), ACT.Copy)
-        turned0 = ps.tile([P, 2, P], F32, name="turned0", tag="early0")
-        turn(picked0[:], turned0[:])
 
         def turn_rows(bank, tile):
             for t in range(PACK):
                 nc.tensor.transpose(bank[:, t, :], tile[:, t, :], ident[:])
+
+        def by_place(col, count):
+            return col[:].unsqueeze(1).to_broadcast([P, count, PACK])
+
+        def by_row(bank):
+            return bank.rearrange("p t q -> p q t")
+
+        turned0 = turn(gather_on_scalar(0), 0, "early0")
 
         row_inv = [sb.tile([P, 1], F32, name=f"row_inv{h}") for h in range(HALVES)]
         rows = [sb.tile([P, PACK, P], F32, name=f"rows{h}", tag="rows", align_bytes=64) for h in range(HALVES)]
@@ -145,125 +157,108 @@ def tile_attend_sinkhorn_pl_kernel(tc, query, keys_words, keys_scales, fac, vals
         turn_rows(slots[0], rows[0])
         nc.vector.reciprocal(row_inv[1][:], row_sum[1][:])
         grouped0 = sb.tile([P, I], BF16, name="grouped0", tag="neg_max1", align_bytes=64)
-        group(grouped0[:], turned0[:], nc.vector.tensor_copy)
+        group(grouped0, turned0, nc.vector.tensor_copy)
+
         both = after_sums.tile([P, PACK, P], F32, name="both", offset=0, align_bytes=64)
         folded = []
         for a, tag in enumerate(("scores0", "late0")):
             bank = ps.tile([P, 2, P], F32, name=f"folded{a}", tag=tag)
-            for part in (slice(2 * a, 2 * a + 2),):
-                nc.vector.scalar_tensor_tensor(
-                    both[:, part, :], expd[1][:, part, :], row_inv[1][:], rows[0][:, part, :], ALU.mult, ALU.add
-                )
-                for t in range(part.start, part.stop):
-                    nc.tensor.transpose(bank[:, t - 2 * a, :], both[:, t, :], ident[:])
+            places = slice(2 * a, 2 * a + 2)
+            nc.vector.scalar_tensor_tensor(
+                both[:, places, :], expd[1][:, places, :], row_inv[1][:], rows[0][:, places, :], ALU.mult, ALU.add
+            )
+            for t in range(2):
+                nc.tensor.transpose(bank[:, t, :], both[:, 2 * a + t, :], ident[:])
             folded.append(bank)
 
         nc.gpsimd.tensor_scalar(rows[1][:], expd[1][:], row_inv[1][:], 1.0, ALU.mult, ALU.mult)
         turn_rows(slots[1], rows[1])
 
-        def along_rows(col, count):
-            return col[:].unsqueeze(1).to_broadcast([P, count, PACK])
-
         with_fac = sb.tile([P, AHEAD, PACK], F32, name="with_fac", align_bytes=64)
-        nc.vector.tensor_tensor(
-            with_fac[:], slots[0][:, :, :AHEAD].rearrange("p t q -> p q t"), along_rows(fac_rows, AHEAD), ALU.mult
-        )
+        nc.vector.tensor_tensor(with_fac[:], by_row(slots[0][:, :, :AHEAD]), by_place(fac_rows, AHEAD), ALU.mult)
 
-        picked1 = sb.tile([P, I], BF16, name="picked1", align_bytes=64)
-        nc.scalar.activation(picked1[:], val_pool[1][:].indirect(offsets[:]), ACT.Copy)
-        picked2 = sb.tile([P, I], BF16, name="picked2", align_bytes=64)
-        nc.scalar.activation(picked2[:], val_pool[2][:].indirect(offsets[:]), ACT.Copy)
+        picked1 = gather_on_scalar(1)
+        picked2 = gather_on_scalar(2)
 
         slot_sum = sb.tile([P, PACK], F32, name="slot_sum")
         for a in range(2):
             nc.vector.tensor_reduce(slot_sum[:, 2 * a : 2 * a + 2], folded[a][:], AX.X, ALU.add)
         slot_inv = sb.tile([P, PACK], F32, name="slot_inv")
-        val_mx = quantize(grouped0[:], P, "val0", 0, after_sums)
+        val_mx = [quantize(grouped0[:], "val0", after_sums, 0)]
         nc.vector.reciprocal(slot_inv[:], slot_sum[:])
         slot_gain = sb.tile([P, PACK], F32, name="slot_gain")
         nc.vector.tensor_tensor(slot_gain[:], slot_inv[:], fac_rows[:], ALU.mult)
         weighed = [sb.tile([P, P, PACK], BF16, name=f"weighed{h}", align_bytes=64) for h in range(HALVES)]
-        nc.vector.tensor_tensor(weighed[0][:, :AHEAD, :], with_fac[:], along_rows(slot_inv, AHEAD), ALU.mult)
+        nc.vector.tensor_tensor(weighed[0][:, :AHEAD, :], with_fac[:], by_place(slot_inv, AHEAD), ALU.mult)
         nc.vector.tensor_tensor(
-            weighed[0][:, AHEAD:, :],
-            slots[0][:, :, AHEAD:].rearrange("p t q -> p q t"),
-            along_rows(slot_gain, P - AHEAD),
-            ALU.mult,
+            weighed[0][:, AHEAD:, :], by_row(slots[0][:, :, AHEAD:]), by_place(slot_gain, P - AHEAD), ALU.mult
         )
-        nc.vector.tensor_tensor(weighed[1][:], slots[1][:].rearrange("p t q -> p q t"), along_rows(slot_gain, P), ALU.mult)
+        nc.vector.tensor_tensor(weighed[1][:], by_row(slots[1][:]), by_place(slot_gain, P), ALU.mult)
 
-        turned1 = ps.tile([P, 2, P], F32, name="turned1", tag="scores0")
-        turn(picked1[:], turned1[:])
+        turned1 = turn(picked1, 1, "scores0")
         grouped1 = after2.tile([P, I], BF16, name="grouped1", offset=0, align_bytes=64)
-        group(grouped1[:], turned1[:])
-        turned2 = ps.tile([P, 2, P], F32, name="turned2", tag="scores1")
-        turn(picked2[:], turned2[:])
+        group(grouped1, turned1, nc.scalar.copy)
+        turned2 = turn(picked2, 2, "scores1")
 
         picked3 = sb.tile([P, I], BF16, name="picked3", align_bytes=64)
-        nc.vector.tensor_copy(picked3[:, :SPLIT], val_pool[LAST][:].indirect(offsets[:, : SPLIT // 16]))
-        nc.scalar.activation(picked3[:, SPLIT:], val_pool[LAST][:].indirect(offsets[:, SPLIT // 16 :]), ACT.Copy)
-        turned3 = ps.tile([P, 2, P], F32, name="turned3", tag="scores0")
-        turn(picked3[:], turned3[:])
+        cut = VECTOR_SHARE // LIST_ROWS
+        nc.vector.tensor_copy(picked3[:, :VECTOR_SHARE], val_pool[LAST][:].indirect(offsets[:, :cut]))
+        nc.scalar.activation(picked3[:, VECTOR_SHARE:], val_pool[LAST][:].indirect(offsets[:, cut:]), ACT.Copy)
+        turned3 = turn(picked3, LAST, "scores0")
         grouped2 = after3.tile([P, I], BF16, name="grouped2", offset=0, align_bytes=64)
-        group(grouped2[:], turned2[:])
-        weight_mx = quantize(weighed[0][:].rearrange("p q t -> p (q t)"), P, "weight0")
-        val_mx += quantize(grouped1[:], P, "val1")
-        weight_mx += quantize(weighed[1][:].rearrange("p q t -> p (q t)"), P, "weight1", 1536)
-        val_mx += quantize(grouped2[:], P, "val2")
+        group(grouped2, turned2, nc.scalar.copy)
+        weight_mx = [quantize(flat(weighed[0][:]), "weight0")]
+        val_mx.append(quantize(grouped1[:], "val1"))
+        weight_mx.append(quantize(flat(weighed[1][:]), "weight1", after3, 3 * KIB // 2))
+        val_mx.append(quantize(grouped2[:], "val2"))
 
-        groups = (slice(0, 2), slice(2, 3), slice(3, 4))
         result = [
             [ps.tile([P, js.stop - js.start, P], F32, name=f"{tag}{h}", tag=f"{tag}{h}") for h in range(HALVES)]
-            for js, tag in zip(groups, ("early", "slots", "late"))
+            for js, tag in zip(GROUPS, ("early", "slots", "late"))
         ]
 
         def multiply(g):
             for h in range(HALVES):
-                for j in range(groups[g].start, groups[g].stop):
+                for j in range(GROUPS[g].start, GROUPS[g].stop):
                     nc.tensor.matmul_mx(
-                        out=result[g][h][:, j - groups[g].start, :],
-                        lhsT=val_mx[j][0].bitcast(FP8X4),
-                        lhsT_scale=val_mx[j][1],
-                        rhs=weight_mx[h][0].bitcast(FP8X4),
-                        rhs_scale=weight_mx[h][1],
+                        out=result[g][h][:, j - GROUPS[g].start, :],
+                        lhsT=val_mx[j][0][:].bitcast(FP8X4),
+                        lhsT_scale=val_mx[j][1][:],
+                        rhs=weight_mx[h][0][:].bitcast(FP8X4),
+                        rhs_scale=weight_mx[h][1][:],
                         start=True,
                         stop=True,
                     )
 
         out_rows = out_0.rearrange("(p j) q -> p j q", j=PACK)
-        rounded = after3.tile([P, Q, PACK], BF16, name="rounded", offset=2048, align_bytes=64)
-
-        def hand_out(g, queue):
-            js = groups[g]
-            staged = after3.tile(
-                [P, js.stop - js.start, Q], F32, name=f"staged{g}", offset=4096 + 1024 * js.start, align_bytes=64
-            )
-            for h, copy in enumerate((nc.vector.tensor_copy, nc.scalar.copy)):
-                cols = slice(h * P, (h + 1) * P)
-                copy(rounded[:, cols, js], result[g][h][:].rearrange("p j q -> p q j"))
-                copy(staged[:, :, cols], result[g][h][:])
-            queue.dma_start(out_rows[:, js, :], staged[:])
+        rounded = after3.tile([P, Q, PACK], BF16, name="rounded", offset=2 * KIB, align_bytes=64)
 
         multiply(0)
         multiply(1)
         grouped3 = sb.tile([P, I], BF16, name="grouped3", align_bytes=64)
-        group(grouped3[:], turned3[:])
-        val_mx += quantize(grouped3[:], P, "val3")
+        group(grouped3, turned3, nc.scalar.copy)
+        val_mx.append(quantize(grouped3[:], "val3"))
         multiply(2)
-        hand_out(0, nc.sync)
-        hand_out(1, nc.sync)
-        hand_out(2, nc.sync)
+
+        for g, js in enumerate(GROUPS):
+            staged = after3.tile(
+                [P, js.stop - js.start, Q], F32, name=f"staged{g}", offset=(4 + js.start) * KIB, align_bytes=64
+            )
+            for h, copy in enumerate((nc.vector.tensor_copy, nc.scalar.copy)):
+                cols = slice(h * P, (h + 1) * P)
+                copy(rounded[:, cols, js], by_row(result[g][h][:]))
+                copy(staged[:, :, cols], result[g][h][:])
+            nc.sync.dma_start(out_rows[:, js, :], staged[:])
+
         out_codes = sb.tile([P, Q], U32, name="out_codes", align_bytes=64)
         out_scales = sb.tile([P, Q], U8, name="out_scales", align_bytes=64)
         for h in range(HALVES):
             cols = slice(h * P, (h + 1) * P)
-            nc.vector.quantize_mx(
-                out_codes[:, cols].bitcast(FP8X4), out_scales[:, cols], rounded[:, cols, :].rearrange("p q j -> p (q j)")
-            )
+            nc.vector.quantize_mx(out_codes[:, cols].bitcast(FP8X4), out_scales[:, cols], flat(rounded[:, cols, :]))
         nc.sync.dma_start(out_1[0].rearrange("p c t -> p (c t)").bitcast(I32), out_codes[:].bitcast(I32))
-        for quad in range(4):
+        for quad in range(QUADS):
             queue = nc.sync if quad % 2 == 0 else nc.scalar
             queue.dma_start(
                 out_2[0, 4 * quad : 4 * quad + 4, :].bitcast(I32),
-                out_scales[32 * quad : 32 * quad + 4, :].bitcast(I32),
+                out_scales[QUAD * quad : QUAD * quad + 4, :].bitcast(I32),
             )

@@ -25,9 +25,9 @@ LAST = PACK - 1
 LIST_ROWS = 16
 QUADS, QUAD = 4, 32
 KIB = 1024
-VECTOR_SHARE = 96
+VECTOR_SHARE = 128
 AHEAD = 64
-GROUPS = (slice(0, 2), slice(2, 3), slice(3, 4))
+GROUPS = (slice(0, 1), slice(1, 3), slice(3, 4))
 
 
 def tile_attend_sinkhorn_pl_kernel(tc, query, keys_words, keys_scales, fac, vals, offs, out_0, out_1, out_2):
@@ -208,7 +208,7 @@ def tile_attend_sinkhorn_pl_kernel(tc, query, keys_words, keys_scales, fac, vals
         grouped2 = after3.tile([P, I], BF16, name="grouped2", offset=0, align_bytes=64)
         group(grouped2, turned2, nc.scalar.copy)
         weight_mx = [quantize(flat(weighed[0][:]), "weight0")]
-        val_mx.append(quantize(grouped1[:], "val1"))
+        val_mx.append(quantize(grouped1[:], "val1", after3, KIB))
         weight_mx.append(quantize(flat(weighed[1][:]), "weight1", after3, 3 * KIB // 2))
         val_mx.append(quantize(grouped2[:], "val2"))
 

@@ -25,9 +25,8 @@ LAST = PACK - 1
 LIST_ROWS = 16
 QUADS, QUAD = 4, 32
 KIB = 1024
-VECTOR_SHARE = 128
-AHEAD = 64
-GROUPS = (slice(0, 1), slice(1, 3), slice(3, 4))
+VECTOR_SHARE = 160
+BANKS = (slice(0, PACK, LAST), slice(1, LAST))
 
 
 def tile_attend_sinkhorn_pl_kernel(tc, query, keys_words, keys_scales, fac, vals, offs, out_0, out_1, out_2):
@@ -35,6 +34,7 @@ def tile_attend_sinkhorn_pl_kernel(tc, query, keys_words, keys_scales, fac, vals
     with ExitStack() as ctx:
         sb = ctx.enter_context(tc.tile_pool(name="sb", bufs=1))
         after_sums = ctx.enter_context(tc.tile_pool(name="after_sums", bufs=1))
+        after1 = ctx.enter_context(tc.tile_pool(name="after1", bufs=1))
         after2 = ctx.enter_context(tc.tile_pool(name="after2", bufs=1))
         after3 = ctx.enter_context(tc.tile_pool(name="after3", bufs=1))
         ps = ctx.enter_context(tc.psum_pool(name="ps", bufs=1))
@@ -55,7 +55,7 @@ def tile_attend_sinkhorn_pl_kernel(tc, query, keys_words, keys_scales, fac, vals
         nc.sync.dma_start(query_rows[:], query.rearrange("(p t) q -> p t q", t=PACK))
         val_planes = vals.rearrange("(p j) t -> j p t", j=PACK)
         val_pool = []
-        for j, (pool, place) in enumerate(((sb, None), (sb, None), (after2, 0), (after3, 0))):
+        for j, (pool, place) in enumerate(((sb, None), (after1, 0), (after2, 0), (after3, 0))):
             plane = pool.tile([P, T], F32, name=f"val_pool{j}", offset=place, align_bytes=64)
             nc.sync.dma_start(plane[:], val_planes[j])
             val_pool.append(plane)
@@ -108,7 +108,7 @@ def tile_attend_sinkhorn_pl_kernel(tc, query, keys_words, keys_scales, fac, vals
         expd, row_sum = [], []
         for h in range(HALVES):
             tile = sb.tile([P, PACK, P], F32, name=f"expd{h}", align_bytes=64)
-            col = sb.tile([P, 1], F32, name=f"row_sum{h}", align_bytes=64)
+            col = sb.tile([P, 1], F32, name=f"row_sum{h}", tag=f"row_sum{h}", align_bytes=64)
             nc.scalar.activation(
                 tile[:],
                 scores[h][:].rearrange("p (s t) -> p t s", t=PACK),
@@ -156,8 +156,6 @@ def tile_attend_sinkhorn_pl_kernel(tc, query, keys_words, keys_scales, fac, vals
         nc.vector.tensor_scalar(rows[0][:], expd[0][:], row_inv[0][:], None, ALU.mult)
         turn_rows(slots[0], rows[0])
         nc.vector.reciprocal(row_inv[1][:], row_sum[1][:])
-        grouped0 = sb.tile([P, I], BF16, name="grouped0", tag="neg_max1", align_bytes=64)
-        group(grouped0, turned0, nc.vector.tensor_copy)
 
         both = after_sums.tile([P, PACK, P], F32, name="both", offset=0, align_bytes=64)
         folded = []
@@ -174,10 +172,12 @@ def tile_attend_sinkhorn_pl_kernel(tc, query, keys_words, keys_scales, fac, vals
         nc.gpsimd.tensor_scalar(rows[1][:], expd[1][:], row_inv[1][:], 1.0, ALU.mult, ALU.mult)
         turn_rows(slots[1], rows[1])
 
-        with_fac = sb.tile([P, AHEAD, PACK], F32, name="with_fac", align_bytes=64)
-        nc.vector.tensor_tensor(with_fac[:], by_row(slots[0][:, :, :AHEAD]), by_place(fac_rows, AHEAD), ALU.mult)
+        with_fac = sb.tile([P, P, PACK], F32, name="with_fac", tag="row_sum1", align_bytes=64)
+        nc.vector.tensor_tensor(with_fac[:], by_row(slots[0][:]), by_place(fac_rows, P), ALU.mult)
 
         picked1 = gather_on_scalar(1)
+        grouped0 = after1.tile([P, I], BF16, name="grouped0", offset=0, align_bytes=64)
+        group(grouped0, turned0, nc.scalar.copy)
         picked2 = gather_on_scalar(2)
 
         slot_sum = sb.tile([P, PACK], F32, name="slot_sum")
@@ -189,10 +189,7 @@ def tile_attend_sinkhorn_pl_kernel(tc, query, keys_words, keys_scales, fac, vals
         slot_gain = sb.tile([P, PACK], F32, name="slot_gain")
         nc.vector.tensor_tensor(slot_gain[:], slot_inv[:], fac_rows[:], ALU.mult)
         weighed = [sb.tile([P, P, PACK], BF16, name=f"weighed{h}", align_bytes=64) for h in range(HALVES)]
-        nc.vector.tensor_tensor(weighed[0][:, :AHEAD, :], with_fac[:], by_place(slot_inv, AHEAD), ALU.mult)
-        nc.vector.tensor_tensor(
-            weighed[0][:, AHEAD:, :], by_row(slots[0][:, :, AHEAD:]), by_place(slot_gain, P - AHEAD), ALU.mult
-        )
+        nc.vector.tensor_tensor(weighed[0][:], with_fac[:], by_place(slot_inv, P), ALU.mult)
         nc.vector.tensor_tensor(weighed[1][:], by_row(slots[1][:]), by_place(slot_gain, P), ALU.mult)
 
         turned1 = turn(picked1, 1, "scores0")
@@ -213,42 +210,54 @@ def tile_attend_sinkhorn_pl_kernel(tc, query, keys_words, keys_scales, fac, vals
         val_mx.append(quantize(grouped2[:], "val2"))
 
         result = [
-            [ps.tile([P, js.stop - js.start, P], F32, name=f"{tag}{h}", tag=f"{tag}{h}") for h in range(HALVES)]
-            for js, tag in zip(GROUPS, ("early", "slots", "late"))
+            [ps.tile([P, 2, P], F32, name=f"{tag}{h}", tag=f"{tag}{h}") for h in range(HALVES)]
+            for tag in ("early", "slots")
         ]
 
-        def multiply(g):
-            for h in range(HALVES):
-                for j in range(GROUPS[g].start, GROUPS[g].stop):
-                    nc.tensor.matmul_mx(
-                        out=result[g][h][:, j - GROUPS[g].start, :],
-                        lhsT=val_mx[j][0][:].bitcast(FP8X4),
-                        lhsT_scale=val_mx[j][1][:],
-                        rhs=weight_mx[h][0][:].bitcast(FP8X4),
-                        rhs_scale=weight_mx[h][1][:],
-                        start=True,
-                        stop=True,
-                    )
+        def multiply(j, h, out):
+            nc.tensor.matmul_mx(
+                out=out,
+                lhsT=val_mx[j][0][:].bitcast(FP8X4),
+                lhsT_scale=val_mx[j][1][:],
+                rhs=weight_mx[h][0][:].bitcast(FP8X4),
+                rhs_scale=weight_mx[h][1][:],
+                start=True,
+                stop=True,
+            )
 
         out_rows = out_0.rearrange("(p j) q -> p j q", j=PACK)
         rounded = after3.tile([P, Q, PACK], BF16, name="rounded", offset=2 * KIB, align_bytes=64)
 
-        multiply(0)
-        multiply(1)
+        copies = (nc.vector.tensor_copy, nc.scalar.copy)
+        halves = [slice(h * P, (h + 1) * P) for h in range(HALVES)]
+
+        def store(js, source):
+            staged = after3.tile(
+                [P, js.stop - js.start, Q], F32, name=f"staged{js.start}", offset=(4 + js.start) * KIB, align_bytes=64
+            )
+            for h in range(HALVES):
+                copies[h](staged[:, :, halves[h]], source[h])
+            nc.sync.dma_start(out_rows[:, js, :], staged[:])
+
+        def round_bank(b):
+            for h in range(HALVES):
+                copies[h](rounded[:, halves[h], BANKS[b]], by_row(result[b][h][:]))
+
+        for h in range(HALVES):
+            multiply(0, h, result[0][h][:, 0, :])
+        for h in range(HALVES):
+            for j in (1, 2):
+                multiply(j, h, result[1][h][:, j - 1, :])
         grouped3 = sb.tile([P, I], BF16, name="grouped3", align_bytes=64)
         group(grouped3, turned3, nc.scalar.copy)
         val_mx.append(quantize(grouped3[:], "val3"))
-        multiply(2)
-
-        for g, js in enumerate(GROUPS):
-            staged = after3.tile(
-                [P, js.stop - js.start, Q], F32, name=f"staged{g}", offset=(4 + js.start) * KIB, align_bytes=64
-            )
-            for h, copy in enumerate((nc.vector.tensor_copy, nc.scalar.copy)):
-                cols = slice(h * P, (h + 1) * P)
-                copy(rounded[:, cols, js], by_row(result[g][h][:]))
-                copy(staged[:, :, cols], result[g][h][:])
-            nc.sync.dma_start(out_rows[:, js, :], staged[:])
+        store(slice(0, 1), [result[0][h][:, :1, :] for h in range(HALVES)])
+        for h in range(HALVES):
+            multiply(LAST, h, result[0][h][:, 1, :])
+        round_bank(1)
+        store(slice(1, LAST), [result[1][h][:] for h in range(HALVES)])
+        round_bank(0)
+        store(slice(LAST, PACK), [result[0][h][:, 1:, :] for h in range(HALVES)])
 
         out_codes = sb.tile([P, Q], U32, name="out_codes", align_bytes=64)
         out_scales = sb.tile([P, Q], U8, name="out_scales", align_bytes=64)

@@ -25,7 +25,8 @@ LAST = PACK - 1
 LIST_ROWS = 16
 QUADS, QUAD = 4, 32
 KIB = 1024
-VECTOR_SHARE = 160
+VECTOR_SHARE = 128
+AHEAD = 64
 BANKS = (slice(0, PACK, LAST), slice(1, LAST))
 
 
@@ -34,7 +35,6 @@ def tile_attend_sinkhorn_pl_kernel(tc, query, keys_words, keys_scales, fac, vals
     with ExitStack() as ctx:
         sb = ctx.enter_context(tc.tile_pool(name="sb", bufs=1))
         after_sums = ctx.enter_context(tc.tile_pool(name="after_sums", bufs=1))
-        after1 = ctx.enter_context(tc.tile_pool(name="after1", bufs=1))
         after2 = ctx.enter_context(tc.tile_pool(name="after2", bufs=1))
         after3 = ctx.enter_context(tc.tile_pool(name="after3", bufs=1))
         ps = ctx.enter_context(tc.psum_pool(name="ps", bufs=1))
@@ -55,7 +55,7 @@ def tile_attend_sinkhorn_pl_kernel(tc, query, keys_words, keys_scales, fac, vals
         nc.sync.dma_start(query_rows[:], query.rearrange("(p t) q -> p t q", t=PACK))
         val_planes = vals.rearrange("(p j) t -> j p t", j=PACK)
         val_pool = []
-        for j, (pool, place) in enumerate(((sb, None), (after1, 0), (after2, 0), (after3, 0))):
+        for j, (pool, place) in enumerate(((sb, None), (sb, None), (after2, 0), (after3, 0))):
             plane = pool.tile([P, T], F32, name=f"val_pool{j}", offset=place, align_bytes=64)
             nc.sync.dma_start(plane[:], val_planes[j])
             val_pool.append(plane)
@@ -108,7 +108,7 @@ def tile_attend_sinkhorn_pl_kernel(tc, query, keys_words, keys_scales, fac, vals
         expd, row_sum = [], []
         for h in range(HALVES):
             tile = sb.tile([P, PACK, P], F32, name=f"expd{h}", align_bytes=64)
-            col = sb.tile([P, 1], F32, name=f"row_sum{h}", tag=f"row_sum{h}", align_bytes=64)
+            col = sb.tile([P, 1], F32, name=f"row_sum{h}", align_bytes=64)
             nc.scalar.activation(
                 tile[:],
                 scores[h][:].rearrange("p (s t) -> p t s", t=PACK),
@@ -156,6 +156,8 @@ def tile_attend_sinkhorn_pl_kernel(tc, query, keys_words, keys_scales, fac, vals
         nc.vector.tensor_scalar(rows[0][:], expd[0][:], row_inv[0][:], None, ALU.mult)
         turn_rows(slots[0], rows[0])
         nc.vector.reciprocal(row_inv[1][:], row_sum[1][:])
+        grouped0 = sb.tile([P, I], BF16, name="grouped0", tag="neg_max1", align_bytes=64)
+        group(grouped0, turned0, nc.vector.tensor_copy)
 
         both = after_sums.tile([P, PACK, P], F32, name="both", offset=0, align_bytes=64)
         folded = []
@@ -172,12 +174,10 @@ def tile_attend_sinkhorn_pl_kernel(tc, query, keys_words, keys_scales, fac, vals
         nc.gpsimd.tensor_scalar(rows[1][:], expd[1][:], row_inv[1][:], 1.0, ALU.mult, ALU.mult)
         turn_rows(slots[1], rows[1])
 
-        with_fac = sb.tile([P, P, PACK], F32, name="with_fac", tag="row_sum1", align_bytes=64)
-        nc.vector.tensor_tensor(with_fac[:], by_row(slots[0][:]), by_place(fac_rows, P), ALU.mult)
+        with_fac = sb.tile([P, AHEAD, PACK], F32, name="with_fac", align_bytes=64)
+        nc.vector.tensor_tensor(with_fac[:], by_row(slots[0][:, :, :AHEAD]), by_place(fac_rows, AHEAD), ALU.mult)
 
         picked1 = gather_on_scalar(1)
-        grouped0 = after1.tile([P, I], BF16, name="grouped0", offset=0, align_bytes=64)
-        group(grouped0, turned0, nc.scalar.copy)
         picked2 = gather_on_scalar(2)
 
         slot_sum = sb.tile([P, PACK], F32, name="slot_sum")
@@ -189,7 +189,10 @@ def tile_attend_sinkhorn_pl_kernel(tc, query, keys_words, keys_scales, fac, vals
         slot_gain = sb.tile([P, PACK], F32, name="slot_gain")
         nc.vector.tensor_tensor(slot_gain[:], slot_inv[:], fac_rows[:], ALU.mult)
         weighed = [sb.tile([P, P, PACK], BF16, name=f"weighed{h}", align_bytes=64) for h in range(HALVES)]
-        nc.vector.tensor_tensor(weighed[0][:], with_fac[:], by_place(slot_inv, P), ALU.mult)
+        nc.vector.tensor_tensor(weighed[0][:, :AHEAD, :], with_fac[:], by_place(slot_inv, AHEAD), ALU.mult)
+        nc.vector.tensor_tensor(
+            weighed[0][:, AHEAD:, :], by_row(slots[0][:, :, AHEAD:]), by_place(slot_gain, P - AHEAD), ALU.mult
+        )
         nc.vector.tensor_tensor(weighed[1][:], by_row(slots[1][:]), by_place(slot_gain, P), ALU.mult)
 
         turned1 = turn(picked1, 1, "scores0")

@@ -25,9 +25,8 @@ LAST = PACK - 1
 LIST_ROWS = 16
 QUADS, QUAD = 4, 32
 KIB = 1024
-VECTOR_SHARE = 128
 AHEAD = 64
-BANKS = (slice(0, PACK, LAST), slice(1, LAST))
+PLANE = (0, 1, 3, 2)
 
 
 def tile_attend_sinkhorn_pl_kernel(tc, query, keys_words, keys_scales, fac, vals, offs, out_0, out_1, out_2):
@@ -35,6 +34,7 @@ def tile_attend_sinkhorn_pl_kernel(tc, query, keys_words, keys_scales, fac, vals
     with ExitStack() as ctx:
         sb = ctx.enter_context(tc.tile_pool(name="sb", bufs=1))
         after_sums = ctx.enter_context(tc.tile_pool(name="after_sums", bufs=1))
+        after1 = ctx.enter_context(tc.tile_pool(name="after1", bufs=1))
         after2 = ctx.enter_context(tc.tile_pool(name="after2", bufs=1))
         after3 = ctx.enter_context(tc.tile_pool(name="after3", bufs=1))
         ps = ctx.enter_context(tc.psum_pool(name="ps", bufs=1))
@@ -43,22 +43,22 @@ def tile_attend_sinkhorn_pl_kernel(tc, query, keys_words, keys_scales, fac, vals
         nc.sync.dma_start(key_word_pool[:].bitcast(I32), keys_words[0].bitcast(I32))
         offsets = sb.tile([P, I // LIST_ROWS], U16, name="offsets")
         nc.sync.dma_start(offsets[:], offs)
-
         key_scale_pool = sb.tile([P, T], U8, name="key_scale_pool")
         nc.gpsimd.memset(key_scale_pool[:].bitcast(I32), 0)
-        fac_rows = sb.tile([P, PACK], F32, name="fac_rows")
-        nc.gpsimd.dma_start(fac_rows[:], fac.rearrange("(p t) o -> p (t o)", t=PACK))
         scale_rows = keys_scales[0].bitcast(I32).rearrange("(quad r) c -> r quad c", r=4)
         for r in range(4):
             nc.sync.dma_start(key_scale_pool[r:P:QUAD, :].bitcast(I32), scale_rows[r])
         query_rows = sb.tile([P, PACK, Q], F32, name="query_rows")
         nc.sync.dma_start(query_rows[:], query.rearrange("(p t) q -> p t q", t=PACK))
         val_planes = vals.rearrange("(p j) t -> j p t", j=PACK)
+        fac_rows = sb.tile([P, PACK], F32, name="fac_rows")
         val_pool = []
-        for j, (pool, place) in enumerate(((sb, None), (sb, None), (after2, 0), (after3, 0))):
+        for j, (pool, place) in enumerate(((sb, None), (after1, 0), (after2, 0), (after3, 0))):
             plane = pool.tile([P, T], F32, name=f"val_pool{j}", offset=place, align_bytes=64)
-            nc.sync.dma_start(plane[:], val_planes[j])
+            nc.sync.dma_start(plane[:], val_planes[PLANE[j]])
             val_pool.append(plane)
+            if j == 0:
+                nc.sync.dma_start(fac_rows[:], fac.rearrange("(p t) o -> p (t o)", t=PACK))
 
         ident = sb.tile([P, P], F32, name="ident")
         make_identity(nc, ident[:])
@@ -72,55 +72,8 @@ def tile_attend_sinkhorn_pl_kernel(tc, query, keys_words, keys_scales, fac, vals
         def flat(tile):
             return tile.rearrange("p q t -> p (q t)")
 
-        key_words = sb.tile([P, I], U16, name="key_words", align_bytes=64)
-        nc.vector.tensor_copy(key_words[:], key_word_pool[:].indirect(offsets[:]))
-        key_scales = sb.tile([P, I], U8, name="key_scales", align_bytes=64)
-        nc.vector.tensor_copy(key_scales[:], key_scale_pool[:].indirect(offsets[:]))
-        query_grouped = []
-        for h in range(HALVES):
-            grouped = sb.tile([P, P, PACK], BF16, name=f"query_grouped{h}", align_bytes=64)
-            nc.scalar.activation(
-                grouped[:].rearrange("p (c i) t -> p c t i", i=4),
-                query_rows[:, :, h * P : (h + 1) * P].rearrange("p t (c i) -> p c t i", i=4),
-                ACT.Copy,
-            )
-            query_grouped.append(grouped)
-        query_mx = [quantize(flat(query_grouped[h][:]), f"query{h}") for h in range(HALVES)]
-
-        scores, neg_max = [], []
-        for h in range(HALVES):
-            bank = ps.tile([P, I], F32, name=f"scores{h}", tag=f"scores{h}")
-            nc.tensor.matmul_mx(
-                out=bank[:],
-                lhsT=query_mx[h][0][:].bitcast(FP8X4),
-                lhsT_scale=query_mx[h][1][:],
-                rhs=key_words[:].bitcast(FP4X4),
-                rhs_scale=key_scales[:],
-                start=True,
-                stop=True,
-            )
-            scores.append(bank)
-        for h in range(HALVES):
-            col = sb.tile([P, 1], F32, name=f"neg_max{h}", tag=f"neg_max{h}", align_bytes=64)
-            nc.vector.tensor_reduce(col[:], scores[h][:], AX.X, ALU.max, negate=True)
-            neg_max.append(col)
-
-        expd, row_sum = [], []
-        for h in range(HALVES):
-            tile = sb.tile([P, PACK, P], F32, name=f"expd{h}", align_bytes=64)
-            col = sb.tile([P, 1], F32, name=f"row_sum{h}", align_bytes=64)
-            nc.scalar.activation(
-                tile[:],
-                scores[h][:].rearrange("p (s t) -> p t s", t=PACK),
-                ACT.Exp,
-                bias=neg_max[h][:],
-                accum_out=col[:],
-            )
-            expd.append(tile)
-            row_sum.append(col)
-
-        def gather_on_scalar(j):
-            picked = sb.tile([P, I], BF16, name=f"picked{j}", align_bytes=64)
+        def gather(j):
+            picked = sb.tile([P, I], BF16, name=f"picked{j}", tag=f"picked{j}", align_bytes=64)
             nc.scalar.activation(picked[:], val_pool[j][:].indirect(offsets[:]), ACT.Copy)
             return picked
 
@@ -147,7 +100,48 @@ def tile_attend_sinkhorn_pl_kernel(tc, query, keys_words, keys_scales, fac, vals
         def by_row(bank):
             return bank.rearrange("p t q -> p q t")
 
-        turned0 = turn(gather_on_scalar(0), 0, "early0")
+        key_words = sb.tile([P, I], U16, name="key_words", align_bytes=64)
+        nc.vector.tensor_copy(key_words[:], key_word_pool[:].indirect(offsets[:]))
+        key_scales = sb.tile([P, I], U8, name="key_scales", align_bytes=64)
+        nc.vector.tensor_copy(key_scales[:], key_scale_pool[:].indirect(offsets[:]))
+        scores, neg_max, expd, row_sum = [], [], [], []
+        for h in range(HALVES):
+            grouped = sb.tile([P, P, PACK], BF16, name=f"query_grouped{h}", align_bytes=64)
+            nc.scalar.activation(
+                grouped[:].rearrange("p (c i) t -> p c t i", i=4),
+                query_rows[:, :, h * P : (h + 1) * P].rearrange("p t (c i) -> p c t i", i=4),
+                ACT.Copy,
+            )
+            codes, scales = quantize(flat(grouped[:]), f"query{h}")
+            bank = ps.tile([P, I], F32, name=f"scores{h}", tag=f"scores{h}")
+            nc.tensor.matmul_mx(
+                out=bank[:],
+                lhsT=codes[:].bitcast(FP8X4),
+                lhsT_scale=scales[:],
+                rhs=key_words[:].bitcast(FP4X4),
+                rhs_scale=key_scales[:],
+                start=True,
+                stop=True,
+            )
+            scores.append(bank)
+        for h in range(HALVES):
+            col = sb.tile([P, 1], F32, name=f"neg_max{h}", align_bytes=64)
+            nc.vector.tensor_reduce(col[:], scores[h][:], AX.X, ALU.max, negate=True)
+            neg_max.append(col)
+        for h in range(HALVES):
+            tile = sb.tile([P, PACK, P], F32, name=f"expd{h}", align_bytes=64)
+            col = sb.tile([P, 1], F32, name=f"row_sum{h}", tag=f"row_sum{h}", align_bytes=64)
+            nc.scalar.activation(
+                tile[:],
+                scores[h][:].rearrange("p (s t) -> p t s", t=PACK),
+                ACT.Exp,
+                bias=neg_max[h][:],
+                accum_out=col[:],
+            )
+            expd.append(tile)
+            row_sum.append(col)
+
+        turned0 = turn(gather(0), 0, "early0")
 
         row_inv = [sb.tile([P, 1], F32, name=f"row_inv{h}") for h in range(HALVES)]
         rows = [sb.tile([P, PACK, P], F32, name=f"rows{h}", tag="rows", align_bytes=64) for h in range(HALVES)]
@@ -156,12 +150,10 @@ def tile_attend_sinkhorn_pl_kernel(tc, query, keys_words, keys_scales, fac, vals
         nc.vector.tensor_scalar(rows[0][:], expd[0][:], row_inv[0][:], None, ALU.mult)
         turn_rows(slots[0], rows[0])
         nc.vector.reciprocal(row_inv[1][:], row_sum[1][:])
-        grouped0 = sb.tile([P, I], BF16, name="grouped0", tag="neg_max1", align_bytes=64)
-        group(grouped0, turned0, nc.vector.tensor_copy)
 
         both = after_sums.tile([P, PACK, P], F32, name="both", offset=0, align_bytes=64)
         folded = []
-        for a, tag in enumerate(("scores0", "late0")):
+        for a, tag in enumerate(("scores0", "spare0")):
             bank = ps.tile([P, 2, P], F32, name=f"folded{a}", tag=tag)
             places = slice(2 * a, 2 * a + 2)
             nc.vector.scalar_tensor_tensor(
@@ -174,11 +166,13 @@ def tile_attend_sinkhorn_pl_kernel(tc, query, keys_words, keys_scales, fac, vals
         nc.gpsimd.tensor_scalar(rows[1][:], expd[1][:], row_inv[1][:], 1.0, ALU.mult, ALU.mult)
         turn_rows(slots[1], rows[1])
 
-        with_fac = sb.tile([P, AHEAD, PACK], F32, name="with_fac", align_bytes=64)
+        with_fac = sb.tile([P, AHEAD, PACK], F32, name="with_fac", tag="row_sum1", align_bytes=64)
         nc.vector.tensor_tensor(with_fac[:], by_row(slots[0][:, :, :AHEAD]), by_place(fac_rows, AHEAD), ALU.mult)
 
-        picked1 = gather_on_scalar(1)
-        picked2 = gather_on_scalar(2)
+        picked1 = gather(1)
+        grouped0 = after1.tile([P, I], BF16, name="grouped0", offset=0, align_bytes=64)
+        group(grouped0, turned0, nc.scalar.copy)
+        picked2 = gather(2)
 
         slot_sum = sb.tile([P, PACK], F32, name="slot_sum")
         for a in range(2):
@@ -188,7 +182,7 @@ def tile_attend_sinkhorn_pl_kernel(tc, query, keys_words, keys_scales, fac, vals
         nc.vector.reciprocal(slot_inv[:], slot_sum[:])
         slot_gain = sb.tile([P, PACK], F32, name="slot_gain")
         nc.vector.tensor_tensor(slot_gain[:], slot_inv[:], fac_rows[:], ALU.mult)
-        weighed = [sb.tile([P, P, PACK], BF16, name=f"weighed{h}", align_bytes=64) for h in range(HALVES)]
+        weighed = [sb.tile([P, P, PACK], BF16, name=f"weighed{h}", tag=f"weighed{h}", align_bytes=64) for h in range(HALVES)]
         nc.vector.tensor_tensor(weighed[0][:, :AHEAD, :], with_fac[:], by_place(slot_inv, AHEAD), ALU.mult)
         nc.vector.tensor_tensor(
             weighed[0][:, AHEAD:, :], by_row(slots[0][:, :, AHEAD:]), by_place(slot_gain, P - AHEAD), ALU.mult
@@ -199,23 +193,16 @@ def tile_attend_sinkhorn_pl_kernel(tc, query, keys_words, keys_scales, fac, vals
         grouped1 = after2.tile([P, I], BF16, name="grouped1", offset=0, align_bytes=64)
         group(grouped1, turned1, nc.scalar.copy)
         turned2 = turn(picked2, 2, "scores1")
+        picked3 = gather(LAST)
 
-        picked3 = sb.tile([P, I], BF16, name="picked3", align_bytes=64)
-        cut = VECTOR_SHARE // LIST_ROWS
-        nc.vector.tensor_copy(picked3[:, :VECTOR_SHARE], val_pool[LAST][:].indirect(offsets[:, :cut]))
-        nc.scalar.activation(picked3[:, VECTOR_SHARE:], val_pool[LAST][:].indirect(offsets[:, cut:]), ACT.Copy)
-        turned3 = turn(picked3, LAST, "scores0")
-        grouped2 = after3.tile([P, I], BF16, name="grouped2", offset=0, align_bytes=64)
-        group(grouped2, turned2, nc.scalar.copy)
         weight_mx = [quantize(flat(weighed[0][:]), "weight0")]
-        val_mx.append(quantize(grouped1[:], "val1", after3, KIB))
-        weight_mx.append(quantize(flat(weighed[1][:]), "weight1", after3, 3 * KIB // 2))
-        val_mx.append(quantize(grouped2[:], "val2"))
+        val_mx.append(quantize(grouped1[:], "val1"))
+        weight_mx.append(quantize(flat(weighed[1][:]), "weight1"))
+        grouped2 = sb.tile([P, I], BF16, name="grouped2", tag="weighed0", align_bytes=64)
+        group(grouped2, turned2, nc.vector.tensor_copy)
 
-        result = [
-            [ps.tile([P, 2, P], F32, name=f"{tag}{h}", tag=f"{tag}{h}") for h in range(HALVES)]
-            for tag in ("early", "slots")
-        ]
+        shared = [ps.tile([P, LAST, P], F32, name=f"shared{h}", tag=f"early{h}") for h in range(HALVES)]
+        alone = [ps.tile([P, 1, P], F32, name=f"alone{h}", tag=f"slots{h}") for h in range(HALVES)]
 
         def multiply(j, h, out):
             nc.tensor.matmul_mx(
@@ -229,8 +216,10 @@ def tile_attend_sinkhorn_pl_kernel(tc, query, keys_words, keys_scales, fac, vals
             )
 
         out_rows = out_0.rearrange("(p j) q -> p j q", j=PACK)
-        rounded = after3.tile([P, Q, PACK], BF16, name="rounded", offset=2 * KIB, align_bytes=64)
-
+        rounded = [
+            sb.tile([P, P, PACK], BF16, name="rounded0", tag="grouped3", align_bytes=64),
+            sb.tile([P, P, PACK], BF16, name="rounded1", tag="picked3", align_bytes=64),
+        ]
         copies = (nc.vector.tensor_copy, nc.scalar.copy)
         halves = [slice(h * P, (h + 1) * P) for h in range(HALVES)]
 
@@ -242,31 +231,34 @@ def tile_attend_sinkhorn_pl_kernel(tc, query, keys_words, keys_scales, fac, vals
                 copies[h](staged[:, :, halves[h]], source[h])
             nc.sync.dma_start(out_rows[:, js, :], staged[:])
 
-        def round_bank(b):
+        def round_places(js, banks):
             for h in range(HALVES):
-                copies[h](rounded[:, halves[h], BANKS[b]], by_row(result[b][h][:]))
+                copies[h](rounded[h][:, :, js], by_row(banks[h][:]))
 
         for h in range(HALVES):
-            multiply(0, h, result[0][h][:, 0, :])
+            for k in range(2):
+                multiply(k, h, shared[h][:, k, :])
+        turned3 = turn(picked3, LAST, "scores0")
+        val_mx.append(quantize(grouped2[:], "val2", after3, 2 * KIB))
         for h in range(HALVES):
-            for j in (1, 2):
-                multiply(j, h, result[1][h][:, j - 1, :])
-        grouped3 = sb.tile([P, I], BF16, name="grouped3", align_bytes=64)
+            multiply(2, h, alone[h][:, 0, :])
+        store(slice(0, 2), [bank[:, :2, :] for bank in shared])
+        grouped3 = sb.tile([P, I], BF16, name="grouped3", tag="grouped3", align_bytes=64)
         group(grouped3, turned3, nc.scalar.copy)
         val_mx.append(quantize(grouped3[:], "val3"))
-        store(slice(0, 1), [result[0][h][:, :1, :] for h in range(HALVES)])
         for h in range(HALVES):
-            multiply(LAST, h, result[0][h][:, 1, :])
-        round_bank(1)
-        store(slice(1, LAST), [result[1][h][:] for h in range(HALVES)])
-        round_bank(0)
-        store(slice(LAST, PACK), [result[0][h][:, 1:, :] for h in range(HALVES)])
+            multiply(LAST, h, shared[h][:, 2, :])
+        store(slice(LAST, PACK), [bank[:] for bank in alone])
+        round_places(slice(LAST, PACK), alone)
+        round_places(slice(0, LAST), shared)
+        store(slice(2, LAST), [bank[:, 2:, :] for bank in shared])
 
         out_codes = sb.tile([P, Q], U32, name="out_codes", align_bytes=64)
         out_scales = sb.tile([P, Q], U8, name="out_scales", align_bytes=64)
         for h in range(HALVES):
-            cols = slice(h * P, (h + 1) * P)
-            nc.vector.quantize_mx(out_codes[:, cols].bitcast(FP8X4), out_scales[:, cols], flat(rounded[:, cols, :]))
+            nc.vector.quantize_mx(
+                out_codes[:, halves[h]].bitcast(FP8X4), out_scales[:, halves[h]], flat(rounded[h][:])
+            )
         nc.sync.dma_start(out_1[0].rearrange("p c t -> p (c t)").bitcast(I32), out_codes[:].bitcast(I32))
         for quad in range(QUADS):
             queue = nc.sync if quad % 2 == 0 else nc.scalar

@@ -25,8 +25,9 @@ LAST = PACK - 1
 LIST_ROWS = 16
 QUADS, QUAD = 4, 32
 KIB = 1024
+VECTOR_SHARE = 128
 AHEAD = 64
-PLANE = (0, 1, 3, 2)
+BANKS = (slice(0, PACK, LAST), slice(1, LAST))
 
 
 def tile_attend_sinkhorn_pl_kernel(tc, query, keys_words, keys_scales, fac, vals, offs, out_0, out_1, out_2):
@@ -55,7 +56,7 @@ def tile_attend_sinkhorn_pl_kernel(tc, query, keys_words, keys_scales, fac, vals
         val_pool = []
         for j, (pool, place) in enumerate(((sb, None), (after1, 0), (after2, 0), (after3, 0))):
             plane = pool.tile([P, T], F32, name=f"val_pool{j}", offset=place, align_bytes=64)
-            nc.sync.dma_start(plane[:], val_planes[PLANE[j]])
+            nc.sync.dma_start(plane[:], val_planes[j])
             val_pool.append(plane)
             if j == 0:
                 nc.sync.dma_start(fac_rows[:], fac.rearrange("(p t) o -> p (t o)", t=PACK))
@@ -67,13 +68,13 @@ def tile_attend_sinkhorn_pl_kernel(tc, query, keys_words, keys_scales, fac, vals
             codes = pool.tile([P, P], U32, name=f"{name}_codes", offset=place, align_bytes=64)
             scales = sb.tile([P, P], U8, name=f"{name}_scales", align_bytes=64)
             nc.vector.quantize_mx(codes[:].bitcast(FP8X4), scales[:], grouped)
-            return codes, scales
+            return codes[:], scales[:]
 
         def flat(tile):
             return tile.rearrange("p q t -> p (q t)")
 
         def gather(j):
-            picked = sb.tile([P, I], BF16, name=f"picked{j}", tag=f"picked{j}", align_bytes=64)
+            picked = sb.tile([P, I], BF16, name=f"picked{j}", align_bytes=64)
             nc.scalar.activation(picked[:], val_pool[j][:].indirect(offsets[:]), ACT.Copy)
             return picked
 
@@ -86,7 +87,7 @@ def tile_attend_sinkhorn_pl_kernel(tc, query, keys_words, keys_scales, fac, vals
 
         def group(grouped, turned, copy):
             copy(
-                grouped[:].bitcast(F32).rearrange("p (e u) -> p e u", u=2),
+                grouped.bitcast(F32).rearrange("p (e u) -> p e u", u=2),
                 turned[:].rearrange("p u e -> p e u"),
             )
 
@@ -116,21 +117,22 @@ def tile_attend_sinkhorn_pl_kernel(tc, query, keys_words, keys_scales, fac, vals
             bank = ps.tile([P, I], F32, name=f"scores{h}", tag=f"scores{h}")
             nc.tensor.matmul_mx(
                 out=bank[:],
-                lhsT=codes[:].bitcast(FP8X4),
-                lhsT_scale=scales[:],
+                lhsT=codes.bitcast(FP8X4),
+                lhsT_scale=scales,
                 rhs=key_words[:].bitcast(FP4X4),
                 rhs_scale=key_scales[:],
                 start=True,
                 stop=True,
             )
             scores.append(bank)
+
         for h in range(HALVES):
             col = sb.tile([P, 1], F32, name=f"neg_max{h}", align_bytes=64)
             nc.vector.tensor_reduce(col[:], scores[h][:], AX.X, ALU.max, negate=True)
             neg_max.append(col)
         for h in range(HALVES):
             tile = sb.tile([P, PACK, P], F32, name=f"expd{h}", align_bytes=64)
-            col = sb.tile([P, 1], F32, name=f"row_sum{h}", tag=f"row_sum{h}", align_bytes=64)
+            col = sb.tile([P, 1], F32, name=f"row_sum{h}", align_bytes=64)
             nc.scalar.activation(
                 tile[:],
                 scores[h][:].rearrange("p (s t) -> p t s", t=PACK),
@@ -163,54 +165,64 @@ def tile_attend_sinkhorn_pl_kernel(tc, query, keys_words, keys_scales, fac, vals
                 nc.tensor.transpose(bank[:, t, :], both[:, 2 * a + t, :], ident[:])
             folded.append(bank)
 
-        nc.gpsimd.tensor_scalar(rows[1][:], expd[1][:], row_inv[1][:], 1.0, ALU.mult, ALU.mult)
+        nc.vector.tensor_scalar(rows[1][:], expd[1][:], row_inv[1][:], None, ALU.mult)
         turn_rows(slots[1], rows[1])
-
-        with_fac = sb.tile([P, AHEAD, PACK], F32, name="with_fac", tag="row_sum1", align_bytes=64)
-        nc.vector.tensor_tensor(with_fac[:], by_row(slots[0][:, :, :AHEAD]), by_place(fac_rows, AHEAD), ALU.mult)
 
         picked1 = gather(1)
         grouped0 = after1.tile([P, I], BF16, name="grouped0", offset=0, align_bytes=64)
-        group(grouped0, turned0, nc.scalar.copy)
+        group(grouped0[:], turned0, nc.scalar.copy)
         picked2 = gather(2)
 
         slot_sum = sb.tile([P, PACK], F32, name="slot_sum")
         for a in range(2):
             nc.vector.tensor_reduce(slot_sum[:, 2 * a : 2 * a + 2], folded[a][:], AX.X, ALU.add)
         slot_inv = sb.tile([P, PACK], F32, name="slot_inv")
-        val_mx = [quantize(grouped0[:], "val0", after_sums, 0)]
+        with_fac = after_sums.tile([P, AHEAD, PACK], F32, name="with_fac", offset=0, align_bytes=64)
+        nc.vector.tensor_tensor(with_fac[:], by_row(slots[0][:, :, :AHEAD]), by_place(fac_rows, AHEAD), ALU.mult)
         nc.vector.reciprocal(slot_inv[:], slot_sum[:])
+        val_mx = [quantize(grouped0[:], "val0", after_sums, KIB)]
         slot_gain = sb.tile([P, PACK], F32, name="slot_gain")
         nc.vector.tensor_tensor(slot_gain[:], slot_inv[:], fac_rows[:], ALU.mult)
-        weighed = [sb.tile([P, P, PACK], BF16, name=f"weighed{h}", tag=f"weighed{h}", align_bytes=64) for h in range(HALVES)]
+        weighed = [sb.tile([P, P, PACK], BF16, name=f"weighed{h}", align_bytes=64)[:] for h in range(HALVES)]
         nc.vector.tensor_tensor(weighed[0][:, :AHEAD, :], with_fac[:], by_place(slot_inv, AHEAD), ALU.mult)
         nc.vector.tensor_tensor(
             weighed[0][:, AHEAD:, :], by_row(slots[0][:, :, AHEAD:]), by_place(slot_gain, P - AHEAD), ALU.mult
         )
-        nc.vector.tensor_tensor(weighed[1][:], by_row(slots[1][:]), by_place(slot_gain, P), ALU.mult)
 
         turned1 = turn(picked1, 1, "scores0")
         grouped1 = after2.tile([P, I], BF16, name="grouped1", offset=0, align_bytes=64)
-        group(grouped1, turned1, nc.scalar.copy)
-        turned2 = turn(picked2, 2, "scores1")
-        picked3 = gather(LAST)
+        group(grouped1[:], turned1, nc.scalar.copy)
+        turned2 = turn(picked2, 2, "slots0")
 
-        weight_mx = [quantize(flat(weighed[0][:]), "weight0")]
-        val_mx.append(quantize(grouped1[:], "val1"))
-        weight_mx.append(quantize(flat(weighed[1][:]), "weight1"))
-        grouped2 = sb.tile([P, I], BF16, name="grouped2", tag="weighed0", align_bytes=64)
-        group(grouped2, turned2, nc.vector.tensor_copy)
+        def weigh_second(part):
+            count = part.stop - part.start
+            nc.vector.tensor_tensor(
+                weighed[1][:, part, :], by_row(slots[1][:, :, part]), by_place(slot_gain, count), ALU.mult
+            )
 
-        shared = [ps.tile([P, LAST, P], F32, name=f"shared{h}", tag=f"early{h}") for h in range(HALVES)]
-        alone = [ps.tile([P, 1, P], F32, name=f"alone{h}", tag=f"slots{h}") for h in range(HALVES)]
+        weigh_second(slice(0, P // 2))
+        weight_mx = [quantize(flat(weighed[0]), "weight0")]
+        weigh_second(slice(P // 2, P))
+
+        picked3 = sb.tile([P, I], BF16, name="picked3", tag="picked3", align_bytes=64)
+        cut = VECTOR_SHARE // LIST_ROWS
+        nc.scalar.activation(picked3[:, VECTOR_SHARE:], val_pool[LAST][:].indirect(offsets[:, cut:]), ACT.Copy)
+        nc.vector.tensor_copy(picked3[:, :VECTOR_SHARE], val_pool[LAST][:].indirect(offsets[:, :cut]))
+        grouped2 = after3.tile([P, I], BF16, name="grouped2", offset=0, align_bytes=64)
+        group(grouped2[:], turned2, nc.scalar.copy)
+
+        result = [
+            [ps.tile([P, 2, P], F32, name=f"result{b}{h}", tag=tag) for h, tag in enumerate(tags)]
+            for b, tags in enumerate((("early0", "early1"), ("slots0", "slots1")))
+        ]
 
         def multiply(j, h, out):
             nc.tensor.matmul_mx(
                 out=out,
-                lhsT=val_mx[j][0][:].bitcast(FP8X4),
-                lhsT_scale=val_mx[j][1][:],
-                rhs=weight_mx[h][0][:].bitcast(FP8X4),
-                rhs_scale=weight_mx[h][1][:],
+                lhsT=val_mx[j][0].bitcast(FP8X4),
+                lhsT_scale=val_mx[j][1],
+                rhs=weight_mx[h][0].bitcast(FP8X4),
+                rhs_scale=weight_mx[h][1],
                 start=True,
                 stop=True,
             )
@@ -223,35 +235,37 @@ def tile_attend_sinkhorn_pl_kernel(tc, query, keys_words, keys_scales, fac, vals
         copies = (nc.vector.tensor_copy, nc.scalar.copy)
         halves = [slice(h * P, (h + 1) * P) for h in range(HALVES)]
 
-        def store(js, source):
+        def store(js, source, engines):
             staged = after3.tile(
                 [P, js.stop - js.start, Q], F32, name=f"staged{js.start}", offset=(4 + js.start) * KIB, align_bytes=64
             )
             for h in range(HALVES):
-                copies[h](staged[:, :, halves[h]], source[h])
+                engines[h](staged[:, :, halves[h]], source[h])
             nc.sync.dma_start(out_rows[:, js, :], staged[:])
 
-        def round_places(js, banks):
+        def round_bank(b):
             for h in range(HALVES):
-                copies[h](rounded[h][:, :, js], by_row(banks[h][:]))
+                copies[h](rounded[h][:, :, BANKS[b]], by_row(result[b][h][:]))
 
+        multiply(0, 0, result[0][0][:, 0, :])
+        turned3 = turn(picked3, LAST, "spare0")
+        weight_mx.append(quantize(flat(weighed[1]), "weight1", after3, KIB))
+        val_mx.append(quantize(grouped1[:], "val1", after3, 3 * KIB // 2))
+        multiply(0, 1, result[0][1][:, 0, :])
+        val_mx.append(quantize(grouped2[:], "val2"))
         for h in range(HALVES):
-            for k in range(2):
-                multiply(k, h, shared[h][:, k, :])
-        turned3 = turn(picked3, LAST, "scores0")
-        val_mx.append(quantize(grouped2[:], "val2", after3, 2 * KIB))
-        for h in range(HALVES):
-            multiply(2, h, alone[h][:, 0, :])
-        store(slice(0, 2), [bank[:, :2, :] for bank in shared])
+            for j in (1, 2):
+                multiply(j, h, result[1][h][:, j - 1, :])
         grouped3 = sb.tile([P, I], BF16, name="grouped3", tag="grouped3", align_bytes=64)
-        group(grouped3, turned3, nc.scalar.copy)
+        group(grouped3[:], turned3, nc.scalar.copy)
+        store(slice(0, 1), [result[0][h][:, :1, :] for h in range(HALVES)], (nc.scalar.copy,) * HALVES)
         val_mx.append(quantize(grouped3[:], "val3"))
         for h in range(HALVES):
-            multiply(LAST, h, shared[h][:, 2, :])
-        store(slice(LAST, PACK), [bank[:] for bank in alone])
-        round_places(slice(LAST, PACK), alone)
-        round_places(slice(0, LAST), shared)
-        store(slice(2, LAST), [bank[:, 2:, :] for bank in shared])
+            multiply(LAST, h, result[0][h][:, 1, :])
+        store(slice(1, LAST), [result[1][h][:] for h in range(HALVES)], copies)
+        round_bank(1)
+        round_bank(0)
+        store(slice(LAST, PACK), [result[0][h][:, 1:, :] for h in range(HALVES)], copies)
 
         out_codes = sb.tile([P, Q], U32, name="out_codes", align_bytes=64)
         out_scales = sb.tile([P, Q], U8, name="out_scales", align_bytes=64)

@@ -25,6 +25,7 @@ LAST = PACK - 1
 LIST_ROWS = 16
 QUADS, QUAD = 4, 32
 KIB = 1024
+ROW_ALIGN = 256
 VECTOR_SHARE = 128
 AHEAD = 64
 BANKS = (slice(0, PACK, LAST), slice(1, LAST))
@@ -40,22 +41,22 @@ def tile_attend_sinkhorn_pl_kernel(tc, query, keys_words, keys_scales, fac, vals
         after3 = ctx.enter_context(tc.tile_pool(name="after3", bufs=1))
         ps = ctx.enter_context(tc.psum_pool(name="ps", bufs=1))
 
-        key_word_pool = sb.tile([P, T], U16, name="key_word_pool")
+        key_word_pool = sb.tile([P, T], U16, name="key_word_pool", align_bytes=ROW_ALIGN)
         nc.sync.dma_start(key_word_pool[:].bitcast(I32), keys_words[0].bitcast(I32))
         offsets = sb.tile([P, I // LIST_ROWS], U16, name="offsets")
         nc.sync.dma_start(offsets[:], offs)
-        key_scale_pool = sb.tile([P, T], U8, name="key_scale_pool")
+        key_scale_pool = sb.tile([P, T], U8, name="key_scale_pool", align_bytes=ROW_ALIGN)
         nc.gpsimd.memset(key_scale_pool[:].bitcast(I32), 0)
         scale_rows = keys_scales[0].bitcast(I32).rearrange("(quad r) c -> r quad c", r=4)
         for r in range(4):
             nc.sync.dma_start(key_scale_pool[r:P:QUAD, :].bitcast(I32), scale_rows[r])
-        query_rows = sb.tile([P, PACK, Q], F32, name="query_rows")
+        query_rows = sb.tile([P, PACK, Q], F32, name="query_rows", align_bytes=ROW_ALIGN)
         nc.sync.dma_start(query_rows[:], query.rearrange("(p t) q -> p t q", t=PACK))
         val_planes = vals.rearrange("(p j) t -> j p t", j=PACK)
         fac_rows = sb.tile([P, PACK], F32, name="fac_rows")
         val_pool = []
         for j, (pool, place) in enumerate(((sb, None), (after1, 0), (after2, 0), (after3, 0))):
-            plane = pool.tile([P, T], F32, name=f"val_pool{j}", offset=place, align_bytes=64)
+            plane = pool.tile([P, T], F32, name=f"val_pool{j}", offset=place, align_bytes=ROW_ALIGN)
             nc.sync.dma_start(plane[:], val_planes[j])
             val_pool.append(plane)
             if j == 0:
@@ -267,8 +268,8 @@ def tile_attend_sinkhorn_pl_kernel(tc, query, keys_words, keys_scales, fac, vals
         round_bank(0)
         store(slice(LAST, PACK), [result[0][h][:, 1:, :] for h in range(HALVES)], copies)
 
-        out_codes = sb.tile([P, Q], U32, name="out_codes", align_bytes=64)
-        out_scales = sb.tile([P, Q], U8, name="out_scales", align_bytes=64)
+        out_codes = sb.tile([P, Q], U32, name="out_codes", align_bytes=ROW_ALIGN)
+        out_scales = sb.tile([P, Q], U8, name="out_scales", align_bytes=ROW_ALIGN)
         for h in range(HALVES):
             nc.vector.quantize_mx(
                 out_codes[:, halves[h]].bitcast(FP8X4), out_scales[:, halves[h]], flat(rounded[h][:])

from contextlib import ExitStack

import concourse.mybir as mybir
from concourse.masks import make_identity

D, T, I, Q, E = 512, 2048, 512, 256, 512
FLOPS = 2 * Q * I * D + 2 * E * Q * I

F32 = mybir.dt.float32
BF16 = mybir.dt.bfloat16
I32 = mybir.dt.int32
U32 = mybir.dt.uint32
U16 = mybir.dt.uint16
U8 = mybir.dt.uint8
FP8X4 = mybir.dt.float8_e4m3fn_x4
FP4X4 = mybir.dt.float4_e2m1fn_x4
ACT = mybir.ActivationFunctionType
ALU = mybir.AluOpType
AX = mybir.AxisListType

P = 128
PACK = 4
HALVES = Q // P
LAST = PACK - 1
LIST_ROWS = 16
QUADS, QUAD = 4, 32
KIB = 1024
ROW_ALIGN = 256
VECTOR_SHARE = 128
AHEAD = 64
BANKS = (slice(0, PACK, LAST), slice(1, LAST))


def tile_attend_sinkhorn_pl_kernel(tc, query, keys_words, keys_scales, fac, vals, offs, out_0, out_1, out_2):
    nc = tc.nc
    with ExitStack() as ctx:
        sb = ctx.enter_context(tc.tile_pool(name="sb", bufs=1))
        after_sums = ctx.enter_context(tc.tile_pool(name="after_sums", bufs=1))
        after1 = ctx.enter_context(tc.tile_pool(name="after1", bufs=1))
        after2 = ctx.enter_context(tc.tile_pool(name="after2", bufs=1))
        after3 = ctx.enter_context(tc.tile_pool(name="after3", bufs=1))
        ps = ctx.enter_context(tc.psum_pool(name="ps", bufs=1))

        key_word_pool = sb.tile([P, T], U16, name="key_word_pool", align_bytes=ROW_ALIGN)
        nc.sync.dma_start(key_word_pool[:].bitcast(I32), keys_words[0].bitcast(I32))
        offsets = sb.tile([P, I // LIST_ROWS], U16, name="offsets")
        nc.sync.dma_start(offsets[:], offs)
        key_scale_pool = sb.tile([P, T], U8, name="key_scale_pool", align_bytes=ROW_ALIGN)
        nc.gpsimd.memset(key_scale_pool[:].bitcast(I32), 0)
        scale_rows = keys_scales[0].bitcast(I32).rearrange("(quad r) c -> r quad c", r=4)
        for r in range(4):
            nc.sync.dma_start(key_scale_pool[r:P:QUAD, :].bitcast(I32), scale_rows[r])
        query_rows = sb.tile([P, PACK, Q], F32, name="query_rows", align_bytes=ROW_ALIGN)
        nc.sync.dma_start(query_rows[:], query.rearrange("(p t) q -> p t q", t=PACK))
        val_planes = vals.rearrange("(p j) t -> j p t", j=PACK)
        fac_rows = sb.tile([P, PACK], F32, name="fac_rows")
        val_pool = []
        for j, (pool, place) in enumerate(((sb, None), (after1, 0), (after2, 0), (after3, 0))):
            plane = pool.tile([P, T], F32, name=f"val_pool{j}", offset=place, align_bytes=ROW_ALIGN)
            nc.sync.dma_start(plane[:], val_planes[j])
            val_pool.append(plane)
            if j == 0:
                nc.sync.dma_start(fac_rows[:], fac.rearrange("(p t) o -> p (t o)", t=PACK))

        ident = sb.tile([P, P], F32, name="ident")
        make_identity(nc, ident[:])

        def quantize(grouped, name, pool=sb, place=None):
            codes = pool.tile([P, P], U32, name=f"{name}_codes", offset=place, align_bytes=64)
            scales = sb.tile([P, P], U8, name=f"{name}_scales", align_bytes=64)
            nc.vector.quantize_mx(codes[:].bitcast(FP8X4), scales[:], grouped)
            return codes[:], scales[:]

        def flat(tile):
            return tile.rearrange("p q t -> p (q t)")

        def gather(j):
            picked = sb.tile([P, I], BF16, name=f"picked{j}", align_bytes=64)
            nc.scalar.activation(picked[:], val_pool[j][:].indirect(offsets[:]), ACT.Copy)
            return picked

        def turn(picked, j, tag):
            turned = ps.tile([P, 2, P], F32, name=f"turned{j}", tag=tag)
            pairs = picked[:].bitcast(F32)
            for u in range(2):
                nc.tensor.transpose(turned[:, u, :], pairs[:, u : I // 2 : 2], ident[:])
            return turned

        def group(grouped, turned, copy):
            copy(
                grouped.bitcast(F32).rearrange("p (e u) -> p e u", u=2),
                turned[:].rearrange("p u e -> p e u"),
            )

        def turn_rows(bank, tile):
            for t in range(PACK):
                nc.tensor.transpose(bank[:, t, :], tile[:, t, :], ident[:])

        def by_place(col, count):
            return col[:].unsqueeze(1).to_broadcast([P, count, PACK])

        def by_row(bank):
            return bank.rearrange("p t q -> p q t")

        key_words = sb.tile([P, I], U16, name="key_words", align_bytes=64)
        nc.vector.tensor_copy(key_words[:], key_word_pool[:].indirect(offsets[:]))
        key_scales = sb.tile([P, I], U8, name="key_scales", align_bytes=64)
        nc.vector.tensor_copy(key_scales[:], key_scale_pool[:].indirect(offsets[:]))
        scores, neg_max, expd, row_sum = [], [], [], []
        for h in range(HALVES):
            grouped = sb.tile([P, P, PACK], BF16, name=f"query_grouped{h}", align_bytes=64)
            nc.scalar.activation(
                grouped[:].rearrange("p (c i) t -> p c t i", i=4),
                query_rows[:, :, h * P : (h + 1) * P].rearrange("p t (c i) -> p c t i", i=4),
                ACT.Copy,
            )
            codes, scales = quantize(flat(grouped[:]), f"query{h}")
            bank = ps.tile([P, I], F32, name=f"scores{h}", tag=f"scores{h}")
            nc.tensor.matmul_mx(
                out=bank[:],
                lhsT=codes.bitcast(FP8X4),
                lhsT_scale=scales,
                rhs=key_words[:].bitcast(FP4X4),
                rhs_scale=key_scales[:],
                start=True,
                stop=True,
            )
            scores.append(bank)

        for h in range(HALVES):
            col = sb.tile([P, 1], F32, name=f"neg_max{h}", align_bytes=64)
            nc.vector.tensor_reduce(col[:], scores[h][:], AX.X, ALU.max, negate=True)
            neg_max.append(col)
        for h in range(HALVES):
            tile = sb.tile([P, PACK, P], F32, name=f"expd{h}", align_bytes=64)
            col = sb.tile([P, 1], F32, name=f"row_sum{h}", align_bytes=64)
            nc.scalar.activation(
                tile[:],
                scores[h][:].rearrange("p (s t) -> p t s", t=PACK),
                ACT.Exp,
                bias=neg_max[h][:],
                accum_out=col[:],
            )
            expd.append(tile)
            row_sum.append(col)

        turned0 = turn(gather(0), 0, "early0")

        row_inv = [sb.tile([P, 1], F32, name=f"row_inv{h}") for h in range(HALVES)]
        rows = [sb.tile([P, PACK, P], F32, name=f"rows{h}", tag="rows", align_bytes=64) for h in range(HALVES)]
        slots = [ps.tile([P, PACK, P], F32, name=f"slots{h}", tag=f"slots{h}") for h in range(HALVES)]
        nc.vector.reciprocal(row_inv[0][:], row_sum[0][:])
        nc.vector.tensor_scalar(rows[0][:], expd[0][:], row_inv[0][:], None, ALU.mult)
        turn_rows(slots[0], rows[0])
        nc.vector.reciprocal(row_inv[1][:], row_sum[1][:])

        both = after_sums.tile([P, PACK, P], F32, name="both", offset=0, align_bytes=64)
        folded = []
        for a, tag in enumerate(("scores0", "spare0")):
            bank = ps.tile([P, 2, P], F32, name=f"folded{a}", tag=tag)
            places = slice(2 * a, 2 * a + 2)
            nc.vector.scalar_tensor_tensor(
                both[:, places, :], expd[1][:, places, :], row_inv[1][:], rows[0][:, places, :], ALU.mult, ALU.add
            )
            for t in range(2):
                nc.tensor.transpose(bank[:, t, :], both[:, 2 * a + t, :], ident[:])
            folded.append(bank)

        nc.vector.tensor_scalar(rows[1][:], expd[1][:], row_inv[1][:], None, ALU.mult)
        turn_rows(slots[1], rows[1])

        picked1 = gather(1)
        grouped0 = after1.tile([P, I], BF16, name="grouped0", offset=0, align_bytes=64)
        group(grouped0[:], turned0, nc.scalar.copy)
        picked2 = gather(2)

        slot_sum = sb.tile([P, PACK], F32, name="slot_sum")
        for a in range(2):
            nc.vector.tensor_reduce(slot_sum[:, 2 * a : 2 * a + 2], folded[a][:], AX.X, ALU.add)
        slot_inv = sb.tile([P, PACK], F32, name="slot_inv")
        with_fac = after_sums.tile([P, AHEAD, PACK], F32, name="with_fac", offset=0, align_bytes=64)
        nc.vector.tensor_tensor(with_fac[:], by_row(slots[0][:, :, :AHEAD]), by_place(fac_rows, AHEAD), ALU.mult)
        nc.vector.reciprocal(slot_inv[:], slot_sum[:])
        val_mx = [quantize(grouped0[:], "val0", after_sums, KIB)]
        slot_gain = sb.tile([P, PACK], F32, name="slot_gain")
        nc.vector.tensor_tensor(slot_gain[:], slot_inv[:], fac_rows[:], ALU.mult)
        weighed = [sb.tile([P, P, PACK], BF16, name=f"weighed{h}", align_bytes=64)[:] for h in range(HALVES)]
        nc.vector.tensor_tensor(weighed[0][:, :AHEAD, :], with_fac[:], by_place(slot_inv, AHEAD), ALU.mult)
        nc.vector.tensor_tensor(
            weighed[0][:, AHEAD:, :], by_row(slots[0][:, :, AHEAD:]), by_place(slot_gain, P - AHEAD), ALU.mult
        )

        turned1 = turn(picked1, 1, "scores0")
        grouped1 = after2.tile([P, I], BF16, name="grouped1", offset=0, align_bytes=64)
        group(grouped1[:], turned1, nc.scalar.copy)
        turned2 = turn(picked2, 2, "slots0")

        def weigh_second(part):
            count = part.stop - part.start
            nc.vector.tensor_tensor(
                weighed[1][:, part, :], by_row(slots[1][:, :, part]), by_place(slot_gain, count), ALU.mult
            )

        weigh_second(slice(0, P // 2))
        weight_mx = [quantize(flat(weighed[0]), "weight0")]
        weigh_second(slice(P // 2, P))

        picked3 = sb.tile([P, I], BF16, name="picked3", tag="picked3", align_bytes=64)
        cut = VECTOR_SHARE // LIST_ROWS
        nc.scalar.activation(picked3[:, VECTOR_SHARE:], val_pool[LAST][:].indirect(offsets[:, cut:]), ACT.Copy)
        nc.vector.tensor_copy(picked3[:, :VECTOR_SHARE], val_pool[LAST][:].indirect(offsets[:, :cut]))
        grouped2 = after3.tile([P, I], BF16, name="grouped2", offset=0, align_bytes=64)
        group(grouped2[:], turned2, nc.scalar.copy)

        result = [
            [ps.tile([P, 2, P], F32, name=f"result{b}{h}", tag=tag) for h, tag in enumerate(tags)]
            for b, tags in enumerate((("early0", "early1"), ("slots0", "slots1")))
        ]

        def multiply(j, h, out):
            nc.tensor.matmul_mx(
                out=out,
                lhsT=val_mx[j][0].bitcast(FP8X4),
                lhsT_scale=val_mx[j][1],
                rhs=weight_mx[h][0].bitcast(FP8X4),
                rhs_scale=weight_mx[h][1],
                start=True,
                stop=True,
            )

        out_rows = out_0.rearrange("(p j) q -> p j q", j=PACK)
        rounded = [
            sb.tile([P, P, PACK], BF16, name="rounded0", tag="grouped3", align_bytes=64),
            sb.tile([P, P, PACK], BF16, name="rounded1", tag="picked3", align_bytes=64),
        ]
        copies = (nc.vector.tensor_copy, nc.scalar.copy)
        halves = [slice(h * P, (h + 1) * P) for h in range(HALVES)]

        def store(js, source, engines):
            staged = after3.tile(
                [P, js.stop - js.start, Q], F32, name=f"staged{js.start}", offset=(4 + js.start) * KIB, align_bytes=64
            )
            for h in range(HALVES):
                engines[h](staged[:, :, halves[h]], source[h])
            nc.sync.dma_start(out_rows[:, js, :], staged[:])

        def round_bank(b):
            for h in range(HALVES):
                copies[h](rounded[h][:, :, BANKS[b]], by_row(result[b][h][:]))

        multiply(0, 0, result[0][0][:, 0, :])
        turned3 = turn(picked3, LAST, "spare0")
        weight_mx.append(quantize(flat(weighed[1]), "weight1", after3, KIB))
        val_mx.append(quantize(grouped1[:], "val1", after3, 3 * KIB // 2))
        multiply(0, 1, result[0][1][:, 0, :])
        val_mx.append(quantize(grouped2[:], "val2"))
        for h in range(HALVES):
            for j in (1, 2):
                multiply(j, h, result[1][h][:, j - 1, :])
        grouped3 = sb.tile([P, I], BF16, name="grouped3", tag="grouped3", align_bytes=64)
        group(grouped3[:], turned3, nc.scalar.copy)
        store(slice(0, 1), [result[0][h][:, :1, :] for h in range(HALVES)], (nc.scalar.copy,) * HALVES)
        val_mx.append(quantize(grouped3[:], "val3"))
        for h in range(HALVES):
            multiply(LAST, h, result[0][h][:, 1, :])
        store(slice(1, LAST), [result[1][h][:] for h in range(HALVES)], copies)
        round_bank(1)
        round_bank(0)
        store(slice(LAST, PACK), [result[0][h][:, 1:, :] for h in range(HALVES)], copies)

        out_codes = sb.tile([P, Q], U32, name="out_codes", align_bytes=ROW_ALIGN)
        out_scales = sb.tile([P, Q], U8, name="out_scales", align_bytes=ROW_ALIGN)
        for h in range(HALVES):
            nc.vector.quantize_mx(
                out_codes[:, halves[h]].bitcast(FP8X4), out_scales[:, halves[h]], flat(rounded[h][:])
            )
        nc.sync.dma_start(out_1[0].rearrange("p c t -> p (c t)").bitcast(I32), out_codes[:].bitcast(I32))
        for quad in range(QUADS):
            queue = nc.sync if quad % 2 == 0 else nc.scalar
            queue.dma_start(
                out_2[0, 4 * quad : 4 * quad + 4, :].bitcast(I32),
                out_scales[QUAD * quad : QUAD * quad + 4, :].bitcast(I32),
            )
